import numpy as np, ml_dtypes
CORES = [40,41,42,43,44,45,46,47]
N = 8
import mx_ref
BF = ml_dtypes.bfloat16
def gentries(a):
    return np.ascontiguousarray(a.reshape(8, 16, -1).transpose(0, 2, 1)).reshape(8, -1)
def gtable(e):
    e = np.asarray(e); return np.ascontiguousarray(e.reshape(8, -1, 16).transpose(0, 2, 1)).reshape(128, -1).astype(np.int32)
def gcols(t, e):
    v = np.concatenate([t.reshape(8, 16, -1, 4), np.zeros((8, 16, 1, 4), BF)], axis=2)
    return np.ascontiguousarray(np.stack([v[g][:, e[g]] for g in range(8)])).reshape(128, -1)
def tile(rs):
    return np.stack(rs, axis=2).reshape(128, -1).astype(BF)
def pick(q, e):
    c = np.concatenate([q[0].reshape(128, -1, 4), np.zeros((128, 1, 4), np.uint8)], axis=1); s = np.concatenate([q[1], np.ones((16, 1), np.uint8)], axis=1)
    return (np.ascontiguousarray(c[:, e].reshape(128, -1)), np.ascontiguousarray(s[:, e]))
def join(*qs):
    return (np.concatenate([q[0] for q in qs], axis=1), np.concatenate([q[1] for q in qs], axis=1))
def put(q, e, v):
    c, s = q[0].reshape(128, -1, 4).copy(), q[1].copy(); c[:, e] = v[0].reshape(128, -1, 4); s[:, e] = v[1]
    return (c.reshape(128, -1), s)
def pk(c, s):
    return (np.ascontiguousarray(c), mx_ref.live(s))
def emit(q):
    return q[0], q[1]
def packed(v, rng):
    q = [mx_ref.quantize(np.ascontiguousarray(v[r])) for r in range(N)]
    return np.stack([a for a, b in q]), np.stack([mx_ref.plane(b, rng) for a, b in q])
def values_of_codes():
    e, c = np.zeros((128, 128, 4), np.float32), np.zeros((128, 2, 4), np.uint8)
    e[np.arange(128), np.arange(128), 0] = 1
    c[:127, :, 0] = np.arange(256).reshape(2, 128).T[:127]
    return mx_ref.matmul(mx_ref.quantize(e.reshape(128, 512).astype(BF)), (c.reshape(128, 8), np.full((16, 2), 127, np.uint8))).T.reshape(-1).astype(np.float64)
CODE_VALUE, SCALE_VALUE = values_of_codes(), 2.0 ** (np.arange(256) - 127.0)
def decode(q):
    return (CODE_VALUE[q[0]].reshape(16, 8, -1, 4) * SCALE_VALUE[q[1]][:, None, :, None] + 0.0).reshape(128, -1).astype(np.float32)
def f(rng, *shape):
    return mx_ref.flush((rng.standard_normal(shape, dtype=np.float32) * np.exp2(rng.integers(-2, 3, shape[:-1] + (1,)))).astype(BF))
def wide(rng, *shape, cols=0):
    v = rng.standard_normal(shape, dtype=np.float32) * np.exp2(rng.integers(-12, 13, shape)).astype(np.float32)
    if cols: v *= np.repeat(np.exp2(rng.integers(-cols, cols + 1, shape[:-2] + (1, shape[-1] // 4))) * (rng.random(shape[:-2] + (1, shape[-1] // 4)) > 0.0625), 4, axis=-1).astype(np.float32)
    return mx_ref.flush(v.astype(BF))
C, F = 384, 192
STEP = [1, 2, 4]
def big(v):
    v = v.astype(np.float32)
    v[np.abs(v) < np.float32(2.0 ** -16)] = 0
    return v.astype(BF)
def numbers_of(rng):
    return {"x": big(f(rng, N, 128, 4 * C)), "u": np.array(f(rng, N, 128, 512)), "v": np.array(f(rng, N, 128, 512))}
def stored(q):
    return {k: np.stack([gtable(q[i, r]) for r in range(N)]) for i, k in enumerate(("pl", "dl", "kl"))}
def lists(rng):
    return stored(rng.permuted(np.tile(np.arange(C), (3, N, 8, 1)), axis=3))
def layers(rng):
    return big(f(rng, N, 128, 2048)).reshape(N, 8, 16, 4, 8, 16, 4)
def weights(rng, w):
    c, s = packed(np.ascontiguousarray(w).reshape(N, 128, 2048), rng)
    return {"wc": c, "ws": s}
def deciding(d):
    u = d["u"].reshape(N, 8, 16, 8, 16, 4)
    u[:, :, :, :, :4] = 0
    return u
def setup_inputs(rng):
    return {**numbers_of(rng), **lists(rng), **weights(rng, layers(rng))}
def setup_inputs_ties(rng):
    d = numbers_of(rng)
    o = rng.permutation(N)
    k = rng.integers(-1, 2, (N, 8, C, 4)).astype(np.float32)
    k[o[1]] = 1
    a = np.exp2(rng.integers(-3, 4, 8).astype(np.float32))
    x = d["x"].reshape(N, 8, 16, C, 4)
    x[:, :, 0] = k.astype(BF)
    x[:, :, 4:6] = 0
    x[:, :, 4, :, 0] = 1.96875 * 2.0 ** 5
    x[:, :, 5, :, 0] = 1.125 * 2.0 ** -8
    x[:, :, 8:] = 0
    x[:, :, 8, :, 0] = (-1.125 * a)[None, :, None].astype(BF)
    x[:, :, 10, :, 0] = (-0.0703125 * a)[None, :, None].astype(BF)
    c = np.ones(N, np.float32)
    c[o[0]] = 0
    c[o[2]] = -1
    u = deciding(d)
    w = layers(rng)
    w[:] = 0
    for g in range(8):
        w[:, g, 8, 0, g, 8, 0] = -28.0
        w[:, g, 5, 0, g, 11, 0] = 4.0
        for b in range(4):
            w[:, g, 10, b, g, 9, 0] = -2.0 ** (b - 5)
            u[:, g, 0, g, b, b] = c.astype(BF)
    return {**d, **lists(rng), **weights(rng, w)}
def setup_inputs_near(rng):
    d = numbers_of(rng)
    o = rng.permutation(N) % 4
    x = d["x"].astype(np.float32).reshape(N, 8, 16, C, 4)
    x[:, :, :10] = 0
    u = deciding(d)
    w = layers(rng)
    w[:, :, :10] = 0
    w[:, :, :, :, :, :10] = 0
    for r in range(N):
        k = 2.0 ** -30 if o[r] == 0 else 1.0
        s = rng.integers(-1, 2, (8, C, 4)).astype(np.float64)
        if o[r] == 3:
            x[r] = 0
            x[r, :, 2, :, 0] = 2.0 ** -30
            x[r, :, 7, :, 0] = 2.0 ** -30
            x[r, :, 8] = rng.choice([-1.0, 1.0], (8, C, 4)) * 2.0 ** -29
            x[r, :, 9, :, 0] = 2.0 ** -29
            w[r] = 0
            for g in range(8):
                w[r, g, 7, 0, g, 2, 0] = 32.0
                for b in range(4):
                    w[r, g, 8, b, g, 0, b] = 2.0 ** -10
                    w[r, g, 8, b, g, 1, b] = -2.0 ** -10
                    w[r, g, 0, b, g, 3, b] = 128.0
                    w[r, g, 8, b, g, 5, b] = 2.0 ** -11
                    w[r, g, 0, b, g, 5, b] = 0.5
                    u[r, g, 0, g, b, b] = 1.125 * 2.0 ** -30
                    u[r, g, 1, g, b, b] = 2.0 ** -30
            continue
        if o[r] == 1:
            s *= np.exp2(rng.integers(0, 3, (8, C, 1)).astype(np.float64))
            x[r, :, 0] = 1.125 * s
            x[r, :, 1] = -s
            x[r, :, 7, :, 0] = 1.96875 * 2.0 ** 13
        else:
            x[r, :, 0] = 1.125 * s * k
            x[r, :, 1] = -1.25 * s * k
            x[r, :, 2, :, 0] = k
        for g, j in zip(rng.permutation(8)[:4], [0, C - 1, int(rng.integers(C)), int(rng.integers(C))]): x[r, g, 0, j, 0] = 2.0 ** 30 * rng.choice([-1.0, 1.0])
        for g in range(8):
            for b in range(4):
                u[r, g, 0, g, b, b] = 1.0 if o[r] == 1 else 1.125 * k
                u[r, g, 1, g, b, b] = k
    d["x"] = x.reshape(N, 128, 4 * C).astype(BF)
    return {**d, **lists(rng), **weights(rng, w)}
def setup_inputs_late(rng):
    d = numbers_of(rng)
    o = rng.permutation(N) % 4
    e = np.stack([o & 1, o >> 1, (o + 1) & 1, ((o + 1) >> 1) & 1], axis=1) * 2.0 - 1.0
    d["x"].reshape(N, 8, 16, C, 4)[:, :, 0] = e[:, None, None, :].astype(np.float32).astype(BF)
    u = deciding(d)
    for g in range(8):
        for b in range(4): u[:, g, 0, g, b, b] = 1
    w = layers(rng)
    w[:, :, :, :, :, 0] = (w[:, :, :, :, :, 0].astype(np.float32) * 4).astype(BF)
    return {**d, **lists(rng), **weights(rng, w)}
def setup_inputs_ends(rng):
    d = numbers_of(rng)
    o, e = rng.permutation(N) % 4, rng.permutation(N) % 4
    s = rng.choice([-1.0, 1.0], (N, 128, C, 4))
    s[o == 0] = -1
    s[o == 1] = rng.choice([-1.0, 1.0], (N, 1, C, 1))[o == 1]
    x = s * (0.76 + 0.02 * rng.random((N, 128, C, 4))) * 2.0 ** 30
    x[o == 3] = 2.0 ** -30
    size = np.where(o == 3, 2.0 ** -30, 2.0 ** 30)
    k = np.stack([rng.permutation(8) for r in range(N)])
    a = np.stack([k & 1, (k >> 1) & 1, k >> 2, (k ^ (k >> 1)) & 1], axis=2) * 2.0 - 1.0
    a[k < 2] = 0
    a = a * size[:, None, None]
    deciding(d)[:, :, :, :, :4] = a.astype(np.float32).astype(BF)[:, None, None, :, :, None]
    v = rng.choice([-1.0, 1.0], (N, 128, 512)) * size[:, None, None]
    q = rng.integers(0, C, (3, N, 8, C))
    q[:, e == 0] = C - 1
    q[:, e == 1] = 0
    q[:, e == 1, 7] = C - 1
    q[:, e == 2] = rng.integers(0, 2, (3, 1, 8, C)) * (C - 1)
    w = np.zeros((N, 128, 4, 128, 4), np.float32)
    i = np.arange(128)
    for b in range(4): w[:, i, b, i, b] = np.where(o[:, None] == 3, 128.0, np.where((i >> 4) % 2 == 0, -0.25, 2.0 ** -12)[None, :])
    d["x"] = x.astype(np.float32).reshape(N, 128, 4 * C).astype(BF)
    d["v"] = v.astype(np.float32).astype(BF)
    return {**d, **stored(q), **weights(rng, w.astype(BF))}
def setup_inputs_spread(rng):
    d = setup_inputs(rng)
    d["x"] = big(wide(rng, N, 128, 4 * C, cols=6))
    return d
def check_inputs(d):
    b = []
    for k in ("x", "u", "v"):
        a = np.abs(d[k].astype(np.float32))
        if not (np.isfinite(a).all() and ((a == 0) | (a >= 2.0 ** -30) & (a <= 2.0 ** 30)).all()): b.append("a value of " + k)
    for k in ("pl", "dl", "kl"):
        if not ((d[k] >= 0) & (d[k] < C)).all(): b.append("an entry of " + k)
    none, least, most = [emit(mx_ref.quantize(np.full((128, 16), k, np.float32).astype(BF)))[1][0, 0] for k in (0.0, 2.0 ** -12, 2.0 ** 7)]
    for r in range(N):
        if ((d["wc"][r] == 0x7F) | (d["wc"][r] == 0xFF)).any(): b.append("wc: a code that is no number")
        s = mx_ref.live(d["ws"][r])
        if ((s != none) & ((s < least) | (s > most))).any(): b.append("ws: a scale out of range")
        if (((d["wc"][r].reshape(16, 8, 512, 4) & 0x7F) != 0) & (s == none)[:, None, :, None]).any(): b.append("wc: a code other than zero under the scale of zeros")
    return b
def at(a, e):
    return np.take_along_axis(a, e, axis=1)
def reference(x, u, v, pl, dl, kl, wc, ws):
    qu = [mx_ref.quantize(u[r]) for r in range(N)]
    lay = [pk(wc[r], ws[r]) for r in range(N)]
    drawn = [np.stack([gentries(pl[r]), gentries(dl[r]), gentries(kl[r])]).astype(np.int64) for r in range(N)]
    link = [drawn[r] for r in range(N)]
    now = [x[r] for r in range(N)]
    for step in STEP:
        made = []
        for r in range(N):
            bit = mx_ref.matmul(qu[r], mx_ref.quantize(now[r])).reshape(8, 16, C) > 0
            for j in range(2):
                p, d, k = link[r]
                one, two = at(bit[:, 2 * j], p), at(bit[:, 2 * j + 1], p)
                t = np.where(two, at(p, p), at(d, p))
                there = np.stack([at(p, t), at(d, t), at(k, t)])
                link[r] = np.where(one, there, np.where(two, drawn[r], np.stack([d, k, p])))
            p, d, k = link[r]
            z = ((gcols(now[r], p).astype(np.float32) + gcols(now[r], k).astype(np.float32)) * np.float32(0.5)).astype(BF)
            q = mx_ref.quantize(z)
            made.append(tile([mx_ref.matmul(pick(lay[r], np.arange(128 * b, 128 * b + 128)), q) * np.float32(0.03125) for b in range(4)]))
        new = []
        for r in range(N):
            i = (r - step) % N
            m = at(link[i][2], link[r][0])
            far = gcols(decode(mx_ref.quantize(made[i])).astype(BF), m[:, :F])
            own = gcols(made[r], m[:, F:])
            new.append((now[r].astype(np.float32) + np.concatenate([far, own], axis=1).astype(np.float32)).astype(BF))
        now = new
    y, lk = np.zeros((N, 128, C), np.float32), np.zeros((N, 8, 3 * C), np.float32)
    oc, osc = np.zeros((N, 128, 4 * C), np.uint8), np.zeros((N, 16, C), np.uint8)
    for r in range(N):
        q = mx_ref.quantize(now[r])
        y[r] = mx_ref.matmul(mx_ref.quantize(v[r]), q)
        lk[r] = np.concatenate([link[r][0], link[r][1], link[r][2]], axis=1)
        oc[r], osc[r] = emit(q)
    return {"y": y, "lk": lk, "oc": oc, "osc": osc}

@@ -1,0 +1,415 @@
+from concourse.mybir import dt, AluOpType, ActivationFunctionType
+
+C, F = 384, 192
+STEP = [1, 2, 4]
+BLOCKS = ((0, 256), (256, 384))
+OFF = 512
+BF, F32, F16, U16, I32 = "bfloat16", "float32", "float16", "uint16", "int32"
+X4, U8 = "float8_e4m3fn_x4", "uint8"
+NB, NN = 2688, 2689
+HOLD = F16
+
+
+def sb(n, d):
+    return ("sbuf", [128, n], d)
+
+
+SCRATCH = {
+    "xt": sb(4 * C, BF), "xh": sb(4 * C, BF), "zp": sb(4 * C, BF), "zt": sb(4 * C, BF), "hh": sb(4 * C, BF), "ft": sb(4 * F, BF),
+    "ut": sb(512, BF), "vt": sb(512, BF), "ones": sb(512, BF), "et": sb(2048, BF),
+    "li": sb(3 * C, I32), "lw": sb(24, I32),
+    "ta": sb(2704, BF), "tb": sb(2688, BF), "fr": sb(C, BF), "mr": sb(C, BF), "ppr": sb(C, BF), "dpr": sb(C, BF),
+    "a0": sb(C, BF), "sg1": sb(C, BF), "sg2": sb(C, BF), "sg3": sb(C, BF), "ga": sb(C, BF), "gb": sb(C, BF), "gf": sb(C, BF),
+    "sca": sb(C, BF), "scb": sb(C, BF), "sc2": sb(C, BF), "sc3": sb(C, BF), "scf": sb(C, BF),
+    "scp": sb(C, HOLD), "scx": sb(C, HOLD), "scy": sb(C, HOLD),
+    "itp": sb(2, I32), "itq": sb(2, I32), "itt": sb(C, F32), "itk": sb(24, F32), "itc": sb(24, F32), "itu": sb(32, F32),
+    "qf": sb(8, F32), "dif": sb(C, BF), "mask": sb(C, BF), "keep": sb(C, BF), "m1": sb(C, BF), "m2": sb(C, BF), "mb": sb(C, BF), "ms": sb(C, BF),
+    "c24": sb(24, F32), "l0": sb(24, F32), "q24": sb(8, F32), "q0": sb(8, F32), "dec": sb(8, F32), "thr": sb(8, F32), "bia": sb(8, F32), "lift": sb(8, F32),
+    "pf": sb(24, F32), "df": sb(24, F32), "yc": sb(24, F32), "zd": sb(24, F32), "zc": sb(24, F32),
+    "n0": sb(24, F32), "n1": sb(24, F32), "n2": sb(24, F32), "n3": sb(24, F32), "n4": sb(24, F32), "n5": sb(24, F32), "n6": sb(24, F32),
+    "e0": sb(24, F32), "e1": sb(24, F32), "e2": sb(24, F32), "e3": sb(24, F32), "e4": sb(24, F32), "e5": sb(24, F32), "e6": sb(24, F32),
+    "f0": sb(24, F32), "f1": sb(24, F32), "f2": sb(24, F32),
+    "order": sb(24, U16), "ulist": sb(32, U16),
+    "wp": sb(24, U16), "wk": sb(24, U16), "wm": sb(24, U16), "wi0": sb(24, U16), "wi1": sb(24, U16), "wf": sb(24, U16), "wp1": sb(24, U16),
+    "lkf": sb(3 * C, F32), "yb": sb(C, F32),
+    "uq": sb(128, X4), "us": sb(128, U8), "uqd": sb(512, X4), "usd": sb(512, U8), "vq": sb(128, X4), "vs": sb(128, U8),
+    "eq": sb(512, X4), "es": sb(512, U8), "wq": sb(512, X4), "wss": sb(512, U8),
+    "qx": sb(C, X4), "sx": sb(C, U8), "qz": sb(C, X4), "sz": sb(C, U8),
+}
+for _t in range(3):
+    SCRATCH.update({"qh%d" % _t: sb(F, X4), "sh%d" % _t: sb(F, U8), "lc%d" % _t: sb(F, X4), "ls%d" % _t: sb(F, U8),
+                    "pin%d" % _t: sb(24, U16), "mo%d" % _t: sb(12, U16)})
+PSUM = ["ps%d" % b for b in range(4)] + ["pw%d" % b for b in range(4)]
+SCRATCH.update({n: ("psum", [128, 512], F32) for n in PSUM})
+
+LOADS = ["dx", "du", "dp", "dd", "dk", "dl", "dw", "ds", "dv"]
+STORES = ["so1", "so0", "sy1", "sy0", "sl"]
+SEMAPHORES = (["qv", "qs", "qt", "qg"] + LOADS + STORES
+              + ["%s%d" % (k, t) for t in range(3) for k in ("ap", "am", "ac", "as", "lp", "lm", "lc", "ls")])
+COUNTER = {"v": "qv", "s": "qs", "t": "qt", "g": "qg"}
+
+
+def rank_program(g, core, T, topo):
+    rank = T.rank_of(core)
+    if rank is None:
+        return
+    N = len(T.cores)
+    OP, AF = AluOpType, ActivationFunctionType
+    eng = {"v": g.vector, "s": g.scalar, "t": g.tensor, "g": g, "y": g.sync}
+
+    total, known = {}, {q: {} for q in eng}
+    hist, spans = {}, {}
+
+    def cols(r):
+        k = (r[1], r[2], r[3])
+        if k not in spans:
+            spans[k] = sum(1 << i for i in range(r[1], r[2], r[3]))
+        return spans[k]
+
+    def V(name, a=0, b=None, st=1):
+        return (name, a, SCRATCH[name][1][1] if b is None else b, st)
+
+    def ap(r):
+        return T[r[0]][:, r[1]:r[2]] if r[3] == 1 else T[r[0]][:, r[1]:r[2]:r[3]]
+
+    def by(r, off):
+        return ap(r).indirect(ap(off))
+
+    def record(rd, wr, op):
+        for rs, w in ((rd, 0), (wr, 1)):
+            for r in rs:
+                hist.setdefault(r[0], []).append((cols(r), w, op))
+
+    def waits(q, rd, wr, sem):
+        need = {}
+        for rs, w in ((rd, 0), (wr, 1)):
+            for r in rs:
+                m, bank = cols(r), r[0] in PSUM
+                for hm, hw, op in hist.get(r[0], ()):
+                    osem, oval, oq, clock = op
+                    if not (w or hw or (bank and oq != q)) or not (bank or hm & m):
+                        continue
+                    if oq == q and osem == COUNTER.get(q) and not hw:
+                        continue
+                    if osem == sem and sem not in COUNTER.values():
+                        continue
+                    if known[q].get(osem, 0) < oval and need.get(osem, (0, None))[0] < oval:
+                        need[osem] = (oval, clock)
+        for osem in sorted(need):
+            oval = need[osem][0]
+            if any(k != osem and c[1].get(osem, 0) >= oval for k, c in need.items()):
+                continue
+            eng[q].wait_ge(T.sem[osem], oval if osem in COUNTER.values() else total[osem])
+        for osem, (oval, clock) in need.items():
+            for k, v in clock.items():
+                known[q][k] = max(known[q].get(k, 0), v)
+            known[q][osem] = max(known[q].get(osem, 0), oval)
+
+    def do(q, call, rd, wr, sem=None, inc=1):
+        sem = sem or COUNTER[q]
+        waits(q, rd, wr, sem)
+        call(eng[q]).then_inc(T.sem[sem], inc)
+        total[sem] = total.get(sem, 0) + inc
+        clock = dict(known[q])
+        clock[sem] = total[sem]
+        record(rd, wr, (sem, total[sem], q, clock))
+
+    def tsc(out, a, s1, op0, s2=None, op1=None, win=None):
+        rd = [a] + [s for s in (s1, s2, win) if isinstance(s, tuple)]
+        p1 = ap(s1) if isinstance(s1, tuple) else s1
+        src = by(win, a) if win else ap(a)
+        if op1 is None:
+            do("v", lambda e: e.tensor_scalar(ap(out), src, p1, None, op0), rd, [out])
+        else:
+            do("v", lambda e: e.tensor_scalar(ap(out), src, p1, s2, op0, op1), rd, [out])
+
+    def tt(out, a, b, op, off=None):
+        src = by(a, off) if off else ap(a)
+        do("v", lambda e: e.tensor_tensor(ap(out), src, ap(b), op), [a, b] + ([off] if off else []), [out])
+
+    def copy(out, a, off=None):
+        src = by(a, off) if off else ap(a)
+        do("v", lambda e: e.tensor_copy(ap(out), src), [a] + ([off] if off else []), [out])
+
+    def act(out, a, func=AF.Copy, scale=None, off=None, bias=None):
+        src = by(a, off) if off else ap(a)
+        kw = {} if scale is None else {"scale": scale}
+        if bias is not None:
+            kw["bias"] = ap(bias) if isinstance(bias, tuple) else bias
+        do("s", lambda e: e.activation(ap(out), src, func, **kw), [a] + [r for r in (off, bias) if isinstance(r, tuple)], [out])
+
+    def scan(out, a, b, initial, op0, op1):
+        do("v", lambda e: e.tensor_tensor_scan(ap(out), ap(a), ap(b), initial, op0, op1), [a, b], [out])
+
+    def quant(c, s, t):
+        do("v", lambda e: e.quantize_mx(ap(c), ap(s), ap(t)), [t], [c, s])
+
+    def mm(out, c, s, c2, s2):
+        do("t", lambda e: e.matmul_mx(ap(out), ap(c), ap(s), ap(c2), ap(s2), True, True), [c, s, c2, s2], [out])
+
+    def load(q, sem, out, src, name):
+        do(q, lambda e: e.dma_start(out, src), [], [name], sem, 16)
+
+    def store(q, sem, out, src, r):
+        do(q, lambda e: e.dma_start(out, src), [r], [], sem, 16)
+
+    def lay(out, row):
+        scan(out, V("keep"), row, 0.0, OP.mult, OP.add)
+
+    def hold(out, row, m, k):
+        scan(out, row, V(m, row[1] % C, row[1] % C + row[2] - row[1]), k, OP.min, OP.add)
+
+    def last(r):
+        return V(r, 15, C, 16)
+
+    def col(name):
+        return V(name, 0, 1)
+
+    def send(t, kind, dst, out, src, codes=False):
+        rid, pid, _ = topo.addr(dst)
+        o, i = (ap(out).bitcast(dt.uint8), ap(src).bitcast(dt.uint8)) if codes else (ap(out), ap(src))
+        lsem = "l%s%d" % (kind, t)
+        waits("g", [src], [], lsem)
+        g.remote_dma(o, i, T.sem["a%s%d" % (kind, t)], T.sem[lsem], pid, rid, topo.mask(core, dst))
+        total[lsem] = len(topo.engines(core, dst))
+        clock = dict(known["g"])
+        clock[lsem] = total[lsem]
+        record([src], [], (lsem, total[lsem], "r", clock))
+
+    for t in range(3):
+        srank, drank = T.cores[(rank - STEP[t]) % N], T.cores[(rank + STEP[t]) % N]
+        for kind, frm, b in (("p", drank, "pin"), ("m", srank, "mo"), ("c", srank, "lc"), ("s", srank, "ls")):
+            s, n = "a%s%d" % (kind, t), len(topo.engines(frm, core))
+            total[s] = n
+            record([], [V("%s%d" % (b, t))], (s, n, "r", {s: n}))
+
+    load("y", "dl", ap(V("lw")), T.pl[:, :], V("lw"))
+    load("s", "du", ap(V("ut")), T.u[:, :], V("ut"))
+    load("y", "dx", ap(V("xt")), T.x[:, :], V("xt"))
+    for k, (q, sem, inp) in enumerate((("y", "dp", T.pl), ("s", "dd", T.dl), ("y", "dk", T.kl))):
+        r = V("li", k * C, k * C + C)
+        for i in range(16):
+            load(q, sem, T.li[i:128:16, k * C:k * C + C], inp[:, :], r)
+    load("s", "dw", T.wq[:, :].bitcast(dt.uint8), T.wc[:, :], V("wq"))
+    load("s", "ds", ap(V("wss")), T.ws[:, :], V("wss"))
+    load("y", "dv", ap(V("vt")), T.v[:, :], V("vt"))
+
+    def iota(out, pattern, cm, flag=True):
+        kw = {"allow_small_or_imprecise_dtypes": True} if flag else {}
+        do("g", lambda e: e.iota(ap(out), pattern, 0, cm, **kw), [], [out])
+
+    iota(V("itp"), [[0, 2]], 1, False)
+    iota(V("itu"), [[1, 4], [16, 8]], 0)
+    iota(V("itk"), [[1, 24]], 0)
+    iota(V("itt"), [[0, 24], [1, 16]], 0)
+    iota(V("itc"), [[16, 24]], 0)
+    do("v", lambda e: e.memset(ap(V("ones")), 1.0), [], [V("ones")])
+    for b in range(4):
+        o = V("et", 512 * b, 512 * b + 512)
+        do("g", lambda e: e.affine_select(ap(o), ap(V("ones")), [[-1, 512]], OP.is_equal, 0.0, b, 4), [V("ones")], [o])
+    do("v", lambda e: e.memset(T.ta[:, NB:NB + 1], 192.0), [], [V("ta", NB, NB + 1)])
+    do("v", lambda e: e.memset(T.ta[:, NN:2704], 576.0), [], [V("ta", NN, 2704)])
+    tsc(V("itq"), V("itp"), 15, OP.bitwise_and)
+    copy(V("qf", 0, 2), V("itq"))
+    copy(V("ulist"), V("itu"))
+    tsc(col("q24"), col("qf"), 24.0, OP.mult)
+    tsc(V("order"), V("itk"), col("q24"), OP.add)
+    tsc(col("q0"), col("qf"), 0.0, OP.is_equal)
+    tsc(col("dec"), col("q0"), -2.0 * OFF, OP.mult, 192.0 + OFF, OP.add)
+    tsc(col("thr"), col("q0"), 8.0, OP.mult, -3.5, OP.add)
+    tsc(col("bia"), col("q0"), -8.0, OP.mult, 4.0, OP.add)
+    tsc(col("lift"), col("q0"), 2.0 * OFF, OP.mult)
+    tsc(V("dif"), V("itt"), col("qf"), OP.subtract)
+    tsc(V("keep"), V("itt"), 0.0, OP.is_gt)
+    tsc(V("mask"), V("dif"), 0.0, OP.is_equal)
+    tsc(V("m1"), V("dif"), -3.0 * OFF, OP.mult, -1.0 * OFF, OP.add)
+    tsc(V("m2"), V("dif"), 1.0 * OFF, OP.mult, -1.0 * OFF, OP.add)
+    tsc(V("m2"), V("m2"), 0.0, OP.min)
+    tt(V("mb"), V("m1"), V("m2"), OP.max)
+    tsc(last("mb"), last("mb"), col("lift"), OP.add)
+    tsc(V("ms"), V("mb"), 1.0 / 128, OP.mult)
+    tsc(V("c24"), V("itc"), col("qf"), OP.add)
+    tsc(V("l0"), V("c24"), 2.0 * C, OP.add)
+    copy(V("wp"), V("lw"))
+    quant(V("uq"), V("us"), V("ut"))
+    do("v", lambda e: e.tensor_copy(T.uqd[:, 0:512].bitcast(dt.uint32), T.uq[:, 0:128].bitcast(dt.uint32).indirect(T.ulist[:, 0:32])),
+       [V("uq"), V("ulist")], [V("uqd")])
+    act(V("usd"), V("us"), off=V("ulist"))
+
+    def prep(h):
+        a, b4 = (F, 4 * F) if h else (0, 0)
+        x, sx = V("qx", a, a + F), V("sx", a, a + F)
+        quant(x, sx, V("xt", b4, b4 + 4 * F))
+        for i in range(4):
+            mm(V("ps%d" % i, 0, F), V("uqd", 128 * i, 128 * i + 128), V("usd", 128 * i, 128 * i + 128), x, sx)
+        for b in range(4):
+            o, i = V("xh", C * b + a, C * b + a + F), V("xt", b4 + b, b4 + 4 * F, 4)
+            if b < 2:
+                tsc(o, i, 0.5, OP.mult)
+            else:
+                act(o, i, scale=0.5)
+        tsc(V("a0", a, a + F), V("ps0", 0, F), 0.0, OP.is_gt)
+        for i in range(1, 4):
+            if h or i != 2:
+                act(V("sg%d" % i, a, a + F), V("ps%d" % i, 0, F), AF.Sign)
+        if h:
+            for i in (2, 3):
+                hold(V("sc%d" % i, a, a + F), V("sg%d" % i, a, a + F), "ms", 8.0)
+
+    def ahead():
+        act(V("ppr"), V("ta", 0, C), off=V("wp"))
+        act(V("dpr"), V("ta", 2 * C, 3 * C), off=V("wp"))
+        hold(V("scx"), V("ppr"), "mb", 2.0 * OFF)
+        tsc(V("pf"), last("scx"), col("dec"), OP.add)
+        hold(V("scy"), V("dpr"), "mb", 2.0 * OFF)
+        tsc(V("df"), last("scy"), col("dec"), OP.add)
+        tt(V("zd"), V("pf"), V("df"), OP.subtract)
+        tt(V("yc"), V("df"), V("l0"), OP.subtract)
+        tsc(V("zc"), V("zd"), float(C), OP.add)
+
+    def rows(k):
+        tsc(V("ta", 2 * C * k, 2 * C * k + C), V("order"), -192.0, OP.add, win=V("li", C * k, C * k + C))
+
+    def turn():
+        tt(V("ga"), V("a0"), V("mask"), OP.mult, off=V("wp"))
+        act(V("gb"), V("sg1"), off=V("wp"))
+        lay(V("sca"), V("ga"))
+        tsc(V("sg2", 0, F), V("ps2", 0, F), 0.0, OP.is_gt)
+        for i in (2, 3):
+            hold(V("sc%d" % i, 0, F), V("sg%d" % i, 0, F), "ms", 8.0)
+        for i in (0, 1):
+            act(V("e%d" % i), last("sc%d" % (i + 2)), AF.Relu, bias=col("bia"))
+        act(V("e2"), V("e1"), AF.Copy, scale=-767.0, bias=2.0 * C - NN)
+        act(V("e3"), V("e1"), AF.Copy, scale=-1.0)
+        hold(V("scb"), V("gb"), "ms", 8.0)
+        tsc(V("n0"), last("scb"), col("thr"), OP.is_ge)
+        tt(V("n1"), V("n0"), V("zc"), OP.mult)
+        tsc(V("n2"), V("n0"), -1.0 * C, OP.mult)
+        tt(V("n3"), V("n1"), V("yc"), OP.add)
+        tt(V("n4"), V("n2"), V("l0"), OP.add)
+        tt(V("n5"), last("sca"), V("n3"), OP.mult)
+        tt(V("n6"), V("n5"), V("n4"), OP.add)
+        copy(V("wi0"), V("n6"))
+        tt(V("e4"), V("n6"), V("e2"), OP.add)
+        tt(V("e5"), V("e0"), V("e4"), OP.mult)
+        tt(V("e6"), V("e5"), V("e3"), OP.add)
+        tsc(V("wf"), V("e6"), 1.0 * NN, OP.add)
+        copy(V("tb", 0, C), V("ta", 0, 3 * C), off=V("wi0"))
+        act(V("fr"), V("ta", 0, 2704), off=V("wf"))
+        act(V("tb", 2 * C, 3 * C), V("ta", 2 * C, 5 * C), off=V("wi0"))
+        hold(V("scp"), V("tb", 0, C), "mb", 2.0 * OFF)
+        tsc(V("wp1"), last("scp"), col("dec"), OP.add)
+        act(V("tb", 4 * C, 5 * C), V("ta", 4 * C, 7 * C), off=V("wi0"))
+        act(V("tb", 6 * C, 7 * C), V("tb", 0, C))
+        tt(V("gf"), V("fr"), V("mask"), OP.mult, off=V("wp1"))
+        lay(V("scf"), V("gf"))
+        tsc(V("f0"), last("scf"), 192.0, OP.is_ge)
+        tt(V("f1"), V("f0"), V("c24"), OP.mult)
+        tt(V("f2"), last("scf"), V("f1"), OP.add)
+        tsc(V("wi1"), V("f2"), 192.0, OP.add)
+        copy(V("ta", 0, C), V("tb", 0, 3 * C), off=V("wi1"))
+        act(V("ta", 4 * C, 5 * C), V("tb", 4 * C, 7 * C), off=V("wi1"))
+        hold(V("scp"), V("ta", 0, C), "mb", 2.0 * OFF)
+        tsc(V("wp"), last("scp"), col("dec"), OP.add)
+
+    for k in range(2):
+        rows(k)
+    prep(1)
+    prep(0)
+    ahead()
+    copy(V("ta", C, 2 * C), V("ta", 0, C))
+    copy(V("ta", 3 * C, 4 * C), V("ta", 2 * C, 3 * C))
+    rows(2)
+    copy(V("ta", 6 * C, 7 * C), V("ta", 0, C))
+    copy(V("ta", 5 * C, 6 * C), V("ta", 4 * C, 5 * C))
+
+    for t in range(3):
+        src, dst = T.cores[(rank - STEP[t]) % N], T.cores[(rank + STEP[t]) % N]
+        turn_first = t == 0
+        if turn_first:
+            for k in range(3):
+                act(V("tb", C + 2 * C * k, 2 * C + 2 * C * k), V("ta", C + 2 * C * k, 2 * C + 2 * C * k))
+        turn()
+        send(t, "p", src, V("pin%d" % t), V("wp"))
+        hold(V("scx"), V("ta", 4 * C, 5 * C), "mb", 2.0 * OFF)
+        tsc(V("wk"), last("scx"), col("dec"), OP.add)
+
+        def zpart(lo, hi):
+            for b in range(4):
+                z, x = V("zp", 4 * lo + (hi - lo) * b, 4 * lo + (hi - lo) * (b + 1)), V("xh", C * b, C * b + C)
+                act(z, x, off=V("wp", lo // 16, hi // 16))
+                tt(V("zt", 4 * lo + b, 4 * hi, 4), x, z, OP.add, off=V("wk", lo // 16, hi // 16))
+            quant(V("qz", lo, hi), V("sz", lo, hi), V("zt", 4 * lo, 4 * hi))
+
+        def wpart(lo, hi):
+            for b in range(4):
+                mm(V("pw%d" % b, 0, hi - lo), V("wq", 128 * b, 128 * b + 128), V("wss", 128 * b, 128 * b + 128), V("qz", lo, hi), V("sz", lo, hi))
+
+        def hpart(lo, hi, b, on):
+            o, i = V("hh", C * b + lo, C * b + hi), V("pw%d" % b, 0, hi - lo)
+            if on == "v":
+                tsc(o, i, 0.03125, OP.mult)
+            else:
+                act(o, i, scale=0.03125)
+
+        zpart(*BLOCKS[0])
+        wpart(*BLOCKS[0])
+        zpart(*BLOCKS[1])
+        act(V("mr"), V("ta", 4 * C, 5 * C), off=V("pin%d" % t))
+        for b in range(4):
+            hpart(*BLOCKS[0], b, "v" if b == 3 else "s")
+        wpart(*BLOCKS[1])
+        hold(V("scy"), V("mr"), "mb", 2.0 * OFF)
+        tsc(V("wm"), last("scy"), col("dec"), OP.add)
+        send(t, "m", dst, V("mo%d" % t), V("wm", 12, 24))
+        for b in range(4):
+            hpart(*BLOCKS[1], b, "v" if b >= 2 else "s")
+        for b in range(4):
+            o, x, off = V("ft", b, 4 * F, 4), V("hh", C * b, C * b + C), V("wm", 0, 12)
+            if b >= 2:
+                copy(o, x, off)
+            else:
+                act(o, x, off=off)
+        quant(V("qh%d" % t), V("sh%d" % t), V("ft"))
+        send(t, "c", dst, V("lc%d" % t), V("qh%d" % t), True)
+        send(t, "s", dst, V("ls%d" % t), V("sh%d" % t))
+        act(V("ta", 2 * C, 3 * C), V("tb", 2 * C, 5 * C), off=V("wi1"))
+        if t == 0:
+            quant(V("eq"), V("es"), V("et"))
+        if t < 2:
+            ahead()
+            copy(V("ta", 6 * C, 7 * C), V("ta", 0, C))
+        else:
+            quant(V("vq"), V("vs"), V("vt"))
+            for k in (0, 2, 1):
+                tsc(V("lkf", C * k, C * k + C), V("ta", 2 * C * k, 2 * C * k + C), 192.0, OP.add)
+            store("y", "sl", T.lk[:, :], T.lkf[0:128:16, 0:3 * C], V("lkf"))
+        for b in range(4):
+            x = V("xt", 4 * F + b, 4 * C, 4)
+            tt(x, V("hh", C * b, C * b + C), x, OP.add, off=V("mo%d" % t))
+        if t < 2:
+            prep(1)
+        else:
+            quant(V("qx", F, C), V("sx", F, C), V("xt", 4 * F, 4 * C))
+            mm(V("ps1", 0, F), V("vq"), V("vs"), V("qx", F, C), V("sx", F, C))
+            act(V("yb", F, C), V("ps1", 0, F))
+            store("y", "so1", T.oc[:, 4 * F:4 * C], T.qx[:, F:C].bitcast(dt.uint8), V("qx", F, C))
+            for k in range(4):
+                store("y", "so1", T.osc[4 * k:4 * k + 4, F:C], T.sx[32 * k:32 * k + 4, F:C], V("sx", F, C))
+            store("y", "sy1", T.y[:, F:C], ap(V("yb", F, C)), V("yb", F, C))
+        for b in range(4):
+            mm(V("pw%d" % b, 0, F), V("eq", 128 * b, 128 * b + 128), V("es", 128 * b, 128 * b + 128), V("lc%d" % t), V("ls%d" % t))
+        for b in range(4):
+            x = V("xt", b, 4 * F, 4)
+            tt(x, V("pw%d" % b, 0, F), x, OP.add)
+        if t < 2:
+            prep(0)
+    quant(V("qx", 0, F), V("sx", 0, F), V("xt", 0, 4 * F))
+    mm(V("ps0", 0, F), V("vq"), V("vs"), V("qx", 0, F), V("sx", 0, F))
+    act(V("yb", 0, F), V("ps0", 0, F))
+    store("y", "so0", T.oc[:, 0:4 * F], T.qx[:, 0:F].bitcast(dt.uint8), V("qx", 0, F))
+    for k in range(4):
+        store("s" if k % 2 else "y", "so0", T.osc[4 * k:4 * k + 4, 0:F], T.sx[32 * k:32 * k + 4, 0:F], V("sx", 0, F))
+    store("y", "sy0", T.y[:, 0:F], ap(V("yb", 0, F)), V("yb", 0, F))
+    for s in sorted(total):
+        g.wait_ge(T.sem[s], total[s])

@@ -23,8 +23,8 @@ SCRATCH = {
     "sca": sb(C, BF), "scb": sb(C, BF), "sc2": sb(C, BF), "sc3": sb(C, BF), "scf": sb(C, BF),
     "scp": sb(C, HOLD), "scx": sb(C, HOLD), "scy": sb(C, HOLD),
     "itp": sb(2, I32), "itq": sb(2, I32), "itt": sb(C, F32), "itk": sb(24, F32), "itc": sb(24, F32), "itu": sb(32, F32),
-    "qf": sb(8, F32), "dif": sb(C, BF), "mask": sb(C, BF), "keep": sb(C, BF), "m1": sb(C, BF), "m2": sb(C, BF), "mb": sb(C, BF), "ms": sb(C, BF),
-    "c24": sb(24, F32), "l0": sb(24, F32), "q24": sb(8, F32), "q0": sb(8, F32), "dec": sb(8, F32), "thr": sb(8, F32), "bia": sb(8, F32), "lift": sb(8, F32),
+    "qf": sb(16, F32), "dif": sb(C, BF), "mask": sb(C, BF), "keep": sb(C, BF), "m1": sb(C, BF), "m2": sb(C, BF), "mb": sb(C, BF), "ms": sb(C, BF),
+    "c24": sb(24, F32), "l0": sb(24, F32),
     "pf": sb(24, F32), "df": sb(24, F32), "yc": sb(24, F32), "zd": sb(24, F32), "zc": sb(24, F32),
     "n0": sb(24, F32), "n1": sb(24, F32), "n2": sb(24, F32), "n3": sb(24, F32), "n4": sb(24, F32), "n5": sb(24, F32), "n6": sb(24, F32),
     "e0": sb(24, F32), "e1": sb(24, F32), "e2": sb(24, F32), "e3": sb(24, F32), "e4": sb(24, F32), "e5": sb(24, F32), "e6": sb(24, F32),
@@ -46,6 +46,7 @@ LOADS = ["dx", "du", "dp", "dd", "dk", "dl", "dw", "ds", "dv"]
 STORES = ["so1", "so0", "sy1", "sy0", "sl"]
 SEMAPHORES = (["qv", "qs", "qt", "qg"] + LOADS + STORES
               + ["%s%d" % (k, t) for t in range(3) for k in ("ap", "am", "ac", "as", "lp", "lm", "lc", "ls")])
+COLS = ["qf", "qf2", "q24", "q0", "dec", "thr", "bia", "biac", "lift", "nq"]
 COUNTER = {"v": "qv", "s": "qs", "t": "qt", "g": "qg"}
 
 
@@ -157,13 +158,14 @@ def rank_program(g, core, T, topo):
         scan(out, V("keep"), row, 0.0, OP.mult, OP.add)
 
     def hold(out, row, m, k):
-        scan(out, row, V(m, row[1] % C, row[1] % C + row[2] - row[1]), k, OP.min, OP.add)
+        scan(out, row, V(m, row[1] % C, row[1] % C + row[2] - row[1]), k, OP.min, OP.subtract)
 
     def last(r):
         return V(r, 15, C, 16)
 
     def col(name):
-        return V(name, 0, 1)
+        i = COLS.index(name)
+        return V("qf", i, i + 1)
 
     def send(t, kind, dst, out, src, codes=False):
         rid, pid, _ = topo.addr(dst)
@@ -203,14 +205,9 @@ def rank_program(g, core, T, topo):
     iota(V("itk"), [[1, 24]], 0)
     iota(V("itt"), [[0, 24], [1, 16]], 0)
     iota(V("itc"), [[16, 24]], 0)
-    do("v", lambda e: e.memset(ap(V("ones")), 1.0), [], [V("ones")])
-    for b in range(4):
-        o = V("et", 512 * b, 512 * b + 512)
-        do("g", lambda e: e.affine_select(ap(o), ap(V("ones")), [[-1, 512]], OP.is_equal, 0.0, b, 4), [V("ones")], [o])
-    do("v", lambda e: e.memset(T.ta[:, NB:NB + 1], 192.0), [], [V("ta", NB, NB + 1)])
-    do("v", lambda e: e.memset(T.ta[:, NN:2704], 576.0), [], [V("ta", NN, 2704)])
     tsc(V("itq"), V("itp"), 15, OP.bitwise_and)
     copy(V("qf", 0, 2), V("itq"))
+    tsc(col("nq"), col("qf"), -1.0, OP.mult)
     copy(V("ulist"), V("itu"))
     tsc(col("q24"), col("qf"), 24.0, OP.mult)
     tsc(V("order"), V("itk"), col("q24"), OP.add)
@@ -218,47 +215,58 @@ def rank_program(g, core, T, topo):
     tsc(col("dec"), col("q0"), -2.0 * OFF, OP.mult, 192.0 + OFF, OP.add)
     tsc(col("thr"), col("q0"), 8.0, OP.mult, -3.5, OP.add)
     tsc(col("bia"), col("q0"), -8.0, OP.mult, 4.0, OP.add)
+    tsc(col("biac"), col("q0"), -8.0 * C, OP.mult, 4.0 * C, OP.add)
     tsc(col("lift"), col("q0"), 2.0 * OFF, OP.mult)
-    tsc(V("dif"), V("itt"), col("qf"), OP.subtract)
-    tsc(V("keep"), V("itt"), 0.0, OP.is_gt)
-    tsc(V("mask"), V("dif"), 0.0, OP.is_equal)
-    tsc(V("m1"), V("dif"), -3.0 * OFF, OP.mult, -1.0 * OFF, OP.add)
-    tsc(V("m2"), V("dif"), 1.0 * OFF, OP.mult, -1.0 * OFF, OP.add)
-    tsc(V("m2"), V("m2"), 0.0, OP.min)
-    tt(V("mb"), V("m1"), V("m2"), OP.max)
-    tsc(last("mb"), last("mb"), col("lift"), OP.add)
-    tsc(V("ms"), V("mb"), 1.0 / 128, OP.mult)
-    tsc(V("c24"), V("itc"), col("qf"), OP.add)
-    tsc(V("l0"), V("c24"), 2.0 * C, OP.add)
+    do("v", lambda e: e.memset(ap(V("ones")), 1.0), [], [V("ones")])
+    for b in range(4):
+        o = V("et", 512 * b, 512 * b + 512)
+        do("g", lambda e: e.affine_select(ap(o), ap(V("ones")), [[-1, 512]], OP.is_equal, 0.0, b, 4), [V("ones")], [o])
+    act(V("dif"), V("itt"), AF.Identity, bias=col("nq"))
+    act(V("m1"), V("dif"), scale=3.0 * OFF, bias=1.0 * OFF)
+    act(V("m2"), V("dif"), AF.Relu, scale=-1.0 * OFF, bias=1.0 * OFF)
+    act(V("keep"), V("itt"), AF.Sign)
+    do("v", lambda e: e.memset(T.ta[:, NB:NB + 1], 192.0), [], [V("ta", NB, NB + 1)])
+    do("v", lambda e: e.memset(T.ta[:, NN:2704], 576.0), [], [V("ta", NN, 2704)])
     copy(V("wp"), V("lw"))
     quant(V("uq"), V("us"), V("ut"))
     do("v", lambda e: e.tensor_copy(T.uqd[:, 0:512].bitcast(dt.uint32), T.uq[:, 0:128].bitcast(dt.uint32).indirect(T.ulist[:, 0:32])),
        [V("uq"), V("ulist")], [V("uqd")])
     act(V("usd"), V("us"), off=V("ulist"))
+    def constants():
+        tt(V("mb"), V("m1"), V("m2"), OP.min)
+        tsc(V("mask"), V("dif"), 0.0, OP.is_equal)
+        tsc(V("c24"), V("itc"), col("qf"), OP.add)
+        tsc(last("mb"), last("mb"), col("lift"), OP.subtract)
+        tsc(V("l0"), V("c24"), 2.0 * C, OP.add)
+        tsc(V("ms"), V("mb"), 1.0 / 128, OP.mult)
 
-    def prep(h):
-        a, b4 = (F, 4 * F) if h else (0, 0)
-        x, sx = V("qx", a, a + F), V("sx", a, a + F)
-        quant(x, sx, V("xt", b4, b4 + 4 * F))
+    def prep(a, e, onv, rest=None):
+        x, sx = V("qx", a, e), V("sx", a, e)
+        quant(x, sx, V("xt", 4 * a, 4 * e))
         for i in range(4):
-            mm(V("ps%d" % i, 0, F), V("uqd", 128 * i, 128 * i + 128), V("usd", 128 * i, 128 * i + 128), x, sx)
+            mm(V("ps%d" % i, 0, e - a), V("uqd", 128 * i, 128 * i + 128), V("usd", 128 * i, 128 * i + 128), x, sx)
         for b in range(4):
-            o, i = V("xh", C * b + a, C * b + a + F), V("xt", b4 + b, b4 + 4 * F, 4)
-            if b < 2:
+            o, i = V("xh", C * b + a, C * b + e), V("xt", 4 * a + b, 4 * e, 4)
+            if b in onv:
                 tsc(o, i, 0.5, OP.mult)
             else:
                 act(o, i, scale=0.5)
-        tsc(V("a0", a, a + F), V("ps0", 0, F), 0.0, OP.is_gt)
+        if rest:
+            rest()
+        tsc(V("a0", a, e), V("ps0", 0, e - a), 0.0, OP.is_gt)
         for i in range(1, 4):
-            if h or i != 2:
-                act(V("sg%d" % i, a, a + F), V("ps%d" % i, 0, F), AF.Sign)
-        if h:
-            for i in (2, 3):
-                hold(V("sc%d" % i, a, a + F), V("sg%d" % i, a, a + F), "ms", 8.0)
+            if a or i != 2:
+                act(V("sg%d" % i, a, e), V("ps%d" % i, 0, e - a), AF.Sign)
+
+    def early():
+        for i in (2, 3):
+            hold(V("sc%d" % i, F, C), V("sg%d" % i, F, C), "ms", 8.0)
+
+    def ahead_rows(both=False):
+        (copy if both else act)(V("ppr"), V("ta", 0, C), off=V("wp"))
+        act(V("dpr"), V("ta", 2 * C, 3 * C), off=V("wp"))
 
     def ahead():
-        act(V("ppr"), V("ta", 0, C), off=V("wp"))
-        act(V("dpr"), V("ta", 2 * C, 3 * C), off=V("wp"))
         hold(V("scx"), V("ppr"), "mb", 2.0 * OFF)
         tsc(V("pf"), last("scx"), col("dec"), OP.add)
         hold(V("scy"), V("dpr"), "mb", 2.0 * OFF)
@@ -270,23 +278,30 @@ def rank_program(g, core, T, topo):
     def rows(k):
         tsc(V("ta", 2 * C * k, 2 * C * k + C), V("order"), -192.0, OP.add, win=V("li", C * k, C * k + C))
 
-    def turn():
+    def turn(t):
         tt(V("ga"), V("a0"), V("mask"), OP.mult, off=V("wp"))
         act(V("gb"), V("sg1"), off=V("wp"))
         lay(V("sca"), V("ga"))
-        tsc(V("sg2", 0, F), V("ps2", 0, F), 0.0, OP.is_gt)
+        n = F if t else C
+        tsc(V("sg2", 0, n), V("ps2", 0, n), 0.0, OP.is_gt)
         for i in (2, 3):
-            hold(V("sc%d" % i, 0, F), V("sg%d" % i, 0, F), "ms", 8.0)
+            hold(V("sc%d" % i, 0, n), V("sg%d" % i, 0, n), "ms", 8.0)
         for i in (0, 1):
             act(V("e%d" % i), last("sc%d" % (i + 2)), AF.Relu, bias=col("bia"))
         act(V("e2"), V("e1"), AF.Copy, scale=-767.0, bias=2.0 * C - NN)
         act(V("e3"), V("e1"), AF.Copy, scale=-1.0)
+        if t == 0:
+            ahead()
+            rows(2)
+            copy(V("ta", C, 2 * C), V("ta", 0, C))
+            copy(V("ta", 3 * C, 4 * C), V("ta", 2 * C, 3 * C))
+            act(V("tb", C, 2 * C), V("ta", C, 2 * C))
         hold(V("scb"), V("gb"), "ms", 8.0)
         tsc(V("n0"), last("scb"), col("thr"), OP.is_ge)
         tt(V("n1"), V("n0"), V("zc"), OP.mult)
-        tsc(V("n2"), V("n0"), -1.0 * C, OP.mult)
+        act(V("n2"), last("scb"), AF.Relu, scale=1.0 * C, bias=col("biac"))
         tt(V("n3"), V("n1"), V("yc"), OP.add)
-        tt(V("n4"), V("n2"), V("l0"), OP.add)
+        tt(V("n4"), V("l0"), V("n2"), OP.subtract)
         tt(V("n5"), last("sca"), V("n3"), OP.mult)
         tt(V("n6"), V("n5"), V("n4"), OP.add)
         copy(V("wi0"), V("n6"))
@@ -299,8 +314,14 @@ def rank_program(g, core, T, topo):
         act(V("tb", 2 * C, 3 * C), V("ta", 2 * C, 5 * C), off=V("wi0"))
         hold(V("scp"), V("tb", 0, C), "mb", 2.0 * OFF)
         tsc(V("wp1"), last("scp"), col("dec"), OP.add)
+        if t == 0:
+            copy(V("ta", 6 * C, 7 * C), V("ta", 0, C))
+            copy(V("ta", 5 * C, 6 * C), V("ta", 4 * C, 5 * C))
         act(V("tb", 4 * C, 5 * C), V("ta", 4 * C, 7 * C), off=V("wi0"))
         act(V("tb", 6 * C, 7 * C), V("tb", 0, C))
+        if t == 0:
+            copy(V("tb", 3 * C, 4 * C), V("ta", 3 * C, 4 * C))
+            act(V("tb", 5 * C, 6 * C), V("ta", 5 * C, 6 * C))
         tt(V("gf"), V("fr"), V("mask"), OP.mult, off=V("wp1"))
         lay(V("scf"), V("gf"))
         tsc(V("f0"), last("scf"), 192.0, OP.is_ge)
@@ -312,24 +333,14 @@ def rank_program(g, core, T, topo):
         hold(V("scp"), V("ta", 0, C), "mb", 2.0 * OFF)
         tsc(V("wp"), last("scp"), col("dec"), OP.add)
 
-    for k in range(2):
-        rows(k)
-    prep(1)
-    prep(0)
-    ahead()
-    copy(V("ta", C, 2 * C), V("ta", 0, C))
-    copy(V("ta", 3 * C, 4 * C), V("ta", 2 * C, 3 * C))
-    rows(2)
-    copy(V("ta", 6 * C, 7 * C), V("ta", 0, C))
-    copy(V("ta", 5 * C, 6 * C), V("ta", 4 * C, 5 * C))
+    rows(0)
+    rows(1)
+    ahead_rows()
+    prep(0, C, (0, 1), constants)
 
     for t in range(3):
         src, dst = T.cores[(rank - STEP[t]) % N], T.cores[(rank + STEP[t]) % N]
-        turn_first = t == 0
-        if turn_first:
-            for k in range(3):
-                act(V("tb", C + 2 * C * k, 2 * C + 2 * C * k), V("ta", C + 2 * C * k, 2 * C + 2 * C * k))
-        turn()
+        turn(t)
         send(t, "p", src, V("pin%d" % t), V("wp"))
         hold(V("scx"), V("ta", 4 * C, 5 * C), "mb", 2.0 * OFF)
         tsc(V("wk"), last("scx"), col("dec"), OP.add)
@@ -355,15 +366,15 @@ def rank_program(g, core, T, topo):
         zpart(*BLOCKS[0])
         wpart(*BLOCKS[0])
         zpart(*BLOCKS[1])
-        act(V("mr"), V("ta", 4 * C, 5 * C), off=V("pin%d" % t))
         for b in range(4):
             hpart(*BLOCKS[0], b, "v" if b == 3 else "s")
+        act(V("mr"), V("ta", 4 * C, 5 * C), off=V("pin%d" % t))
         wpart(*BLOCKS[1])
+        for b in range(4):
+            hpart(*BLOCKS[1], b, "s" if b == 3 else "v")
         hold(V("scy"), V("mr"), "mb", 2.0 * OFF)
         tsc(V("wm"), last("scy"), col("dec"), OP.add)
         send(t, "m", dst, V("mo%d" % t), V("wm", 12, 24))
-        for b in range(4):
-            hpart(*BLOCKS[1], b, "v" if b >= 2 else "s")
         for b in range(4):
             o, x, off = V("ft", b, 4 * F, 4), V("hh", C * b, C * b + C), V("wm", 0, 12)
             if b >= 2:
@@ -377,8 +388,7 @@ def rank_program(g, core, T, topo):
         if t == 0:
             quant(V("eq"), V("es"), V("et"))
         if t < 2:
-            ahead()
-            copy(V("ta", 6 * C, 7 * C), V("ta", 0, C))
+            ahead_rows(True)
         else:
             quant(V("vq"), V("vs"), V("vt"))
             for k in (0, 2, 1):
@@ -388,7 +398,9 @@ def rank_program(g, core, T, topo):
             x = V("xt", 4 * F + b, 4 * C, 4)
             tt(x, V("hh", C * b, C * b + C), x, OP.add, off=V("mo%d" % t))
         if t < 2:
-            prep(1)
+            prep(F, C, (), ahead)
+            early()
+            act(V("ta", 6 * C, 7 * C), V("ta", 0, C))
         else:
             quant(V("qx", F, C), V("sx", F, C), V("xt", 4 * F, 4 * C))
             mm(V("ps1", 0, F), V("vq"), V("vs"), V("qx", F, C), V("sx", F, C))
@@ -403,7 +415,7 @@ def rank_program(g, core, T, topo):
             x = V("xt", b, 4 * F, 4)
             tt(x, V("pw%d" % b, 0, F), x, OP.add)
         if t < 2:
-            prep(0)
+            prep(0, F, (0, 1))
     quant(V("qx", 0, F), V("sx", 0, F), V("xt", 0, 4 * F))
     mm(V("ps0", 0, F), V("vq"), V("vs"), V("qx", 0, F), V("sx", 0, F))
     act(V("yb", 0, F), V("ps0", 0, F))

@@ -3,7 +3,7 @@ from concourse.mybir import dt, AluOpType, ActivationFunctionType
 C, F = 384, 192
 STEP = [1, 2, 4]
 BLOCKS = ((0, 256), (256, 384))
-OFF = 512
+OFF = 1024
 BF, F32, F16, U16, I32 = "bfloat16", "float32", "float16", "uint16", "int32"
 X4, U8 = "float8_e4m3fn_x4", "uint8"
 NB, NN = 2688, 2689
@@ -20,10 +20,10 @@ SCRATCH = {
     "li": sb(3 * C, I32), "lw": sb(24, I32),
     "ta": sb(2704, BF), "tb": sb(2688, BF), "fr": sb(C, BF), "mr": sb(C, BF), "ppr": sb(C, BF), "dpr": sb(C, BF),
     "a0": sb(C, BF), "sg1": sb(C, BF), "sg2": sb(C, BF), "sg3": sb(C, BF), "ga": sb(C, BF), "gb": sb(C, BF), "gf": sb(C, BF),
-    "sca": sb(C, BF), "scb": sb(C, BF), "sc2": sb(C, BF), "sc3": sb(C, BF), "scf": sb(C, BF),
+    "sca": sb(C, BF), "scb": sb(C, BF), "sc2": sb(C, BF), "sc3": sb(C, BF), "scf": sb(C, HOLD),
     "scp": sb(C, HOLD), "scx": sb(C, HOLD), "scy": sb(C, HOLD),
     "itp": sb(2, I32), "itq": sb(2, I32), "itt": sb(C, F32), "itk": sb(24, F32), "itc": sb(24, F32), "itu": sb(32, F32),
-    "qf": sb(16, F32), "dif": sb(C, BF), "mask": sb(C, BF), "keep": sb(C, BF), "m1": sb(C, BF), "m2": sb(C, BF), "mb": sb(C, BF), "ms": sb(C, BF),
+    "qf": sb(16, F32), "dif": sb(C, BF), "m1": sb(C, BF), "m2": sb(C, BF), "mb": sb(C, BF), "ms": sb(C, BF),
     "c24": sb(24, F32), "l0": sb(24, F32),
     "pf": sb(24, F32), "df": sb(24, F32), "yc": sb(24, F32), "zd": sb(24, F32), "zc": sb(24, F32),
     "n0": sb(24, F32), "n1": sb(24, F32), "n2": sb(24, F32), "n3": sb(24, F32), "n4": sb(24, F32), "n5": sb(24, F32), "n6": sb(24, F32),
@@ -46,7 +46,7 @@ LOADS = ["dx", "du", "dp", "dd", "dk", "dl", "dw", "ds", "dv"]
 STORES = ["so1", "so0", "sy1", "sy0", "sl"]
 SEMAPHORES = (["qv", "qs", "qt", "qg"] + LOADS + STORES
               + ["%s%d" % (k, t) for t in range(3) for k in ("ap", "am", "ac", "as", "lp", "lm", "lc", "ls")])
-COLS = ["qf", "qf2", "q24", "q0", "dec", "thr", "bia", "biac", "lift", "nq"]
+COLS = ["qf", "qf2", "q24", "q0", "dec", "thr", "bia", "mark", "lift", "lifs", "quarter"]
 COUNTER = {"v": "qv", "s": "qs", "t": "qt", "g": "qg"}
 
 
@@ -154,9 +154,6 @@ def rank_program(g, core, T, topo):
     def store(q, sem, out, src, r):
         do(q, lambda e: e.dma_start(out, src), [r], [], sem, 16)
 
-    def lay(out, row):
-        scan(out, V("keep"), row, 0.0, OP.mult, OP.add)
-
     def hold(out, row, m, k):
         scan(out, row, V(m, row[1] % C, row[1] % C + row[2] - row[1]), k, OP.min, OP.subtract)
 
@@ -192,8 +189,8 @@ def rank_program(g, core, T, topo):
         r = V("li", k * C, k * C + C)
         for i in range(16):
             load(q, sem, T.li[i:128:16, k * C:k * C + C], inp[:, :], r)
-    load("s", "dw", T.wq[:, :].bitcast(dt.uint8), T.wc[:, :], V("wq"))
-    load("s", "ds", ap(V("wss")), T.ws[:, :], V("wss"))
+    load("y", "dw", T.wq[:, :].bitcast(dt.uint8), T.wc[:, :], V("wq"))
+    load("y", "ds", ap(V("wss")), T.ws[:, :], V("wss"))
     load("y", "dv", ap(V("vt")), T.v[:, :], V("vt"))
 
     def iota(out, pattern, cm, flag=True):
@@ -205,40 +202,39 @@ def rank_program(g, core, T, topo):
     iota(V("itk"), [[1, 24]], 0)
     iota(V("itt"), [[0, 24], [1, 16]], 0)
     iota(V("itc"), [[16, 24]], 0)
+    do("v", lambda e: e.memset(ap(V("ones")), 1.0), [], [V("ones")])
+    do("v", lambda e: e.memset(T.ta[:, NB:NB + 1], 192.0), [], [V("ta", NB, NB + 1)])
+    do("v", lambda e: e.memset(T.ta[:, NN:2704], 576.0), [], [V("ta", NN, 2704)])
     tsc(V("itq"), V("itp"), 15, OP.bitwise_and)
     copy(V("qf", 0, 2), V("itq"))
-    tsc(col("nq"), col("qf"), -1.0, OP.mult)
+    tsc(col("quarter"), col("qf"), 0.0, OP.mult, 0.25, OP.add)
+    tsc(col("q0"), col("qf"), 0.0, OP.is_equal)
     copy(V("ulist"), V("itu"))
     tsc(col("q24"), col("qf"), 24.0, OP.mult)
     tsc(V("order"), V("itk"), col("q24"), OP.add)
-    tsc(col("q0"), col("qf"), 0.0, OP.is_equal)
+    tsc(col("lifs"), col("q0"), 8.0, OP.mult)
     tsc(col("dec"), col("q0"), -2.0 * OFF, OP.mult, 192.0 + OFF, OP.add)
     tsc(col("thr"), col("q0"), 8.0, OP.mult, -3.5, OP.add)
     tsc(col("bia"), col("q0"), -8.0, OP.mult, 4.0, OP.add)
-    tsc(col("biac"), col("q0"), -8.0 * C, OP.mult, 4.0 * C, OP.add)
+    tsc(col("mark"), col("q0"), 2.0 * OFF, OP.mult, 191.5 - OFF, OP.add)
     tsc(col("lift"), col("q0"), 2.0 * OFF, OP.mult)
-    do("v", lambda e: e.memset(ap(V("ones")), 1.0), [], [V("ones")])
     for b in range(4):
         o = V("et", 512 * b, 512 * b + 512)
         do("g", lambda e: e.affine_select(ap(o), ap(V("ones")), [[-1, 512]], OP.is_equal, 0.0, b, 4), [V("ones")], [o])
-    act(V("dif"), V("itt"), AF.Identity, bias=col("nq"))
-    act(V("m1"), V("dif"), scale=3.0 * OFF, bias=1.0 * OFF)
-    act(V("m2"), V("dif"), AF.Relu, scale=-1.0 * OFF, bias=1.0 * OFF)
-    act(V("keep"), V("itt"), AF.Sign)
-    do("v", lambda e: e.memset(T.ta[:, NB:NB + 1], 192.0), [], [V("ta", NB, NB + 1)])
-    do("v", lambda e: e.memset(T.ta[:, NN:2704], 576.0), [], [V("ta", NN, 2704)])
+    act(V("m1"), V("itt"), AF.Sign, scale=-1.0, bias=col("qf"))
+    act(V("m2"), V("m1"), AF.Square, bias=col("quarter"))
+    act(V("mb"), V("m2"), scale=-2.0 * OFF, bias=1.125 * OFF)
+    act(V("ms"), V("m2"), scale=-8.0, bias=4.5)
     copy(V("wp"), V("lw"))
     quant(V("uq"), V("us"), V("ut"))
     do("v", lambda e: e.tensor_copy(T.uqd[:, 0:512].bitcast(dt.uint32), T.uq[:, 0:128].bitcast(dt.uint32).indirect(T.ulist[:, 0:32])),
        [V("uq"), V("ulist")], [V("uqd")])
     act(V("usd"), V("us"), off=V("ulist"))
     def constants():
-        tt(V("mb"), V("m1"), V("m2"), OP.min)
-        tsc(V("mask"), V("dif"), 0.0, OP.is_equal)
         tsc(V("c24"), V("itc"), col("qf"), OP.add)
-        tsc(last("mb"), last("mb"), col("lift"), OP.subtract)
+        tsc(last("ms"), last("ms"), col("lifs"), OP.subtract)
         tsc(V("l0"), V("c24"), 2.0 * C, OP.add)
-        tsc(V("ms"), V("mb"), 1.0 / 128, OP.mult)
+        tsc(last("mb"), last("mb"), col("lift"), OP.subtract)
 
     def prep(a, e, onv, rest=None):
         x, sx = V("qx", a, e), V("sx", a, e)
@@ -268,75 +264,79 @@ def rank_program(g, core, T, topo):
 
     def ahead():
         hold(V("scx"), V("ppr"), "mb", 2.0 * OFF)
-        tsc(V("pf"), last("scx"), col("dec"), OP.add)
         hold(V("scy"), V("dpr"), "mb", 2.0 * OFF)
+        tsc(V("pf"), last("scx"), col("dec"), OP.add)
         tsc(V("df"), last("scy"), col("dec"), OP.add)
         tt(V("zd"), V("pf"), V("df"), OP.subtract)
         tt(V("yc"), V("df"), V("l0"), OP.subtract)
         tsc(V("zc"), V("zd"), float(C), OP.add)
 
+    def aside(out, a):
+        do("g", lambda e: e.affine_select(ap(out), ap(a), [[1, C]], OP.is_ge, 0.0, 0, 0), [a], [out])
+
     def rows(k):
         tsc(V("ta", 2 * C * k, 2 * C * k + C), V("order"), -192.0, OP.add, win=V("li", C * k, C * k + C))
 
     def turn(t):
-        tt(V("ga"), V("a0"), V("mask"), OP.mult, off=V("wp"))
+        copy(V("ga"), V("a0"), off=V("wp"))
         act(V("gb"), V("sg1"), off=V("wp"))
-        lay(V("sca"), V("ga"))
         n = F if t else C
-        tsc(V("sg2", 0, n), V("ps2", 0, n), 0.0, OP.is_gt)
-        for i in (2, 3):
-            hold(V("sc%d" % i, 0, n), V("sg%d" % i, 0, n), "ms", 8.0)
+        if t:
+            tsc(V("sg2", 0, n), V("ps2", 0, n), 0.0, OP.is_gt)
+        else:
+            act(V("sg2"), V("ps2", 0, n), AF.Sign)
+            rows(0)
+            rows(1)
+            ahead_rows()
+            rows(2)
+        hold(V("sca"), V("ga"), "ms", 8.0)
+        hold(V("sc2", 0, n), V("sg2", 0, n), "ms", 8.0)
+        tsc(V("n0"), last("sca"), col("thr"), OP.is_ge)
+        hold(V("sc3", 0, n), V("sg3", 0, n), "ms", 8.0)
         for i in (0, 1):
             act(V("e%d" % i), last("sc%d" % (i + 2)), AF.Relu, bias=col("bia"))
         act(V("e2"), V("e1"), AF.Copy, scale=-767.0, bias=2.0 * C - NN)
-        act(V("e3"), V("e1"), AF.Copy, scale=-1.0)
+        act(V("e3"), V("e1"), AF.Copy, scale=-1.0, bias=1.0 * NN)
         if t == 0:
+            for a, b in ((1, 0), (3, 2), (5, 4)):
+                act(V("ta", C * a, C * a + C), V("ta", C * b, C * b + C))
+            for n, a, b in (("ta", 6, 0), ("tb", 1, 0), ("tb", 3, 2), ("tb", 5, 4)):
+                aside(V(n, C * a, C * a + C), V("ta", C * b, C * b + C))
             ahead()
-            rows(2)
-            copy(V("ta", C, 2 * C), V("ta", 0, C))
-            copy(V("ta", 3 * C, 4 * C), V("ta", 2 * C, 3 * C))
-            act(V("tb", C, 2 * C), V("ta", C, 2 * C))
+        tt(V("n1"), V("n0"), V("yc"), OP.mult)
+        tt(V("n2"), V("n0"), V("zc"), OP.mult)
+        tt(V("n3"), V("n1"), V("l0"), OP.add)
+        tsc(V("n4"), V("n2"), -1.0 * C, OP.add)
         hold(V("scb"), V("gb"), "ms", 8.0)
-        tsc(V("n0"), last("scb"), col("thr"), OP.is_ge)
-        tt(V("n1"), V("n0"), V("zc"), OP.mult)
-        act(V("n2"), last("scb"), AF.Relu, scale=1.0 * C, bias=col("biac"))
-        tt(V("n3"), V("n1"), V("yc"), OP.add)
-        tt(V("n4"), V("l0"), V("n2"), OP.subtract)
-        tt(V("n5"), last("sca"), V("n3"), OP.mult)
-        tt(V("n6"), V("n5"), V("n4"), OP.add)
+        tt(V("e4"), V("e0"), V("e2"), OP.mult)
+        tsc(V("n5"), last("scb"), col("thr"), OP.is_ge)
+        tt(V("e5"), V("e4"), V("e3"), OP.add)
+        tt(V("n1"), V("n5"), V("n4"), OP.mult)
+        tt(V("n6"), V("n1"), V("n3"), OP.add)
+        tt(V("e6"), V("e0"), V("n6"), OP.mult)
         copy(V("wi0"), V("n6"))
-        tt(V("e4"), V("n6"), V("e2"), OP.add)
-        tt(V("e5"), V("e0"), V("e4"), OP.mult)
-        tt(V("e6"), V("e5"), V("e3"), OP.add)
-        tsc(V("wf"), V("e6"), 1.0 * NN, OP.add)
+        tt(V("e4"), V("e6"), V("e5"), OP.add)
+        copy(V("wf"), V("e4"))
         copy(V("tb", 0, C), V("ta", 0, 3 * C), off=V("wi0"))
         act(V("fr"), V("ta", 0, 2704), off=V("wf"))
         act(V("tb", 2 * C, 3 * C), V("ta", 2 * C, 5 * C), off=V("wi0"))
         hold(V("scp"), V("tb", 0, C), "mb", 2.0 * OFF)
         tsc(V("wp1"), last("scp"), col("dec"), OP.add)
-        if t == 0:
-            copy(V("ta", 6 * C, 7 * C), V("ta", 0, C))
-            copy(V("ta", 5 * C, 6 * C), V("ta", 4 * C, 5 * C))
+        aside(V("tb", 6 * C, 7 * C), V("tb", 0, C))
         act(V("tb", 4 * C, 5 * C), V("ta", 4 * C, 7 * C), off=V("wi0"))
-        act(V("tb", 6 * C, 7 * C), V("tb", 0, C))
-        if t == 0:
-            copy(V("tb", 3 * C, 4 * C), V("ta", 3 * C, 4 * C))
-            act(V("tb", 5 * C, 6 * C), V("ta", 5 * C, 6 * C))
-        tt(V("gf"), V("fr"), V("mask"), OP.mult, off=V("wp1"))
-        lay(V("scf"), V("gf"))
-        tsc(V("f0"), last("scf"), 192.0, OP.is_ge)
+        copy(V("gf"), V("fr"), off=V("wp1"))
+        hold(V("scf"), V("gf"), "mb", 2.0 * OFF)
+        tsc(V("f0"), last("scf"), col("mark"), OP.is_ge)
         tt(V("f1"), V("f0"), V("c24"), OP.mult)
         tt(V("f2"), last("scf"), V("f1"), OP.add)
-        tsc(V("wi1"), V("f2"), 192.0, OP.add)
+        tsc(V("wi1"), V("f2"), col("dec"), OP.add)
         copy(V("ta", 0, C), V("tb", 0, 3 * C), off=V("wi1"))
         act(V("ta", 4 * C, 5 * C), V("tb", 4 * C, 7 * C), off=V("wi1"))
         hold(V("scp"), V("ta", 0, C), "mb", 2.0 * OFF)
         tsc(V("wp"), last("scp"), col("dec"), OP.add)
 
-    rows(0)
-    rows(1)
-    ahead_rows()
-    prep(0, C, (0, 1), constants)
+    constants()
+    prep(0, C, (0, 1))
 
     for t in range(3):
         src, dst = T.cores[(rank - STEP[t]) % N], T.cores[(rank + STEP[t]) % N]
@@ -368,13 +368,18 @@ def rank_program(g, core, T, topo):
         zpart(*BLOCKS[1])
         for b in range(4):
             hpart(*BLOCKS[0], b, "v" if b == 3 else "s")
-        act(V("mr"), V("ta", 4 * C, 5 * C), off=V("pin%d" % t))
+        for lo, hi in ((F, C), (0, F)):
+            act(V("mr", lo, hi), V("ta", 4 * C, 5 * C), off=V("pin%d" % t, lo // 16, hi // 16))
         wpart(*BLOCKS[1])
-        for b in range(4):
-            hpart(*BLOCKS[1], b, "s" if b == 3 else "v")
-        hold(V("scy"), V("mr"), "mb", 2.0 * OFF)
-        tsc(V("wm"), last("scy"), col("dec"), OP.add)
+        hpart(*BLOCKS[1], 0, "v")
+        hold(V("scy", F, C), V("mr", F, C), "mb", 2.0 * OFF)
+        hpart(*BLOCKS[1], 1, "v")
+        tsc(V("wm", 12, 24), V("scy", F + 15, C, 16), col("dec"), OP.add)
         send(t, "m", dst, V("mo%d" % t), V("wm", 12, 24))
+        hpart(*BLOCKS[1], 2, "v")
+        hold(V("scy", 0, F), V("mr", 0, F), "mb", 2.0 * OFF)
+        tsc(V("wm", 0, 12), V("scy", 15, F, 16), col("dec"), OP.add)
+        hpart(*BLOCKS[1], 3, "s")
         for b in range(4):
             o, x, off = V("ft", b, 4 * F, 4), V("hh", C * b, C * b + C), V("wm", 0, 12)
             if b >= 2:

from concourse.mybir import dt, AluOpType, ActivationFunctionType

C, F = 384, 192
STEP = [1, 2, 4]
BLOCKS = ((0, 256), (256, 384))
OFF = 1024
BF, F32, F16, U16, I32 = "bfloat16", "float32", "float16", "uint16", "int32"
X4, U8 = "float8_e4m3fn_x4", "uint8"
NB, NN = 2688, 2689
HOLD = F16


def sb(n, d):
    return ("sbuf", [128, n], d)


SCRATCH = {
    "xt": sb(4 * C, BF), "xh": sb(4 * C, BF), "zp": sb(4 * C, BF), "zt": sb(4 * C, BF), "hh": sb(4 * C, BF), "ft": sb(4 * F, BF),
    "ut": sb(512, BF), "vt": sb(512, BF), "ones": sb(512, BF), "et": sb(2048, BF),
    "li": sb(3 * C, I32), "lw": sb(24, I32),
    "ta": sb(2704, BF), "tb": sb(2688, BF), "fr": sb(C, BF), "mr": sb(C, BF), "ppr": sb(C, BF), "dpr": sb(C, BF),
    "a0": sb(C, BF), "sg1": sb(C, BF), "sg2": sb(C, BF), "sg3": sb(C, BF), "ga": sb(C, BF), "gb": sb(C, BF), "gf": sb(C, BF),
    "sca": sb(C, BF), "scb": sb(C, BF), "sc2": sb(C, BF), "sc3": sb(C, BF), "scf": sb(C, HOLD),
    "scp": sb(C, HOLD), "scx": sb(C, HOLD), "scy": sb(C, HOLD),
    "itp": sb(2, I32), "itq": sb(2, I32), "itt": sb(C, F32), "itk": sb(24, F32), "itc": sb(24, F32), "itu": sb(32, F32),
    "qf": sb(16, F32), "dif": sb(C, BF), "m1": sb(C, BF), "m2": sb(C, BF), "mb": sb(C, BF), "ms": sb(C, BF),
    "c24": sb(24, F32), "l0": sb(24, F32),
    "pf": sb(24, F32), "df": sb(24, F32), "yc": sb(24, F32), "zd": sb(24, F32), "zc": sb(24, F32),
    "n0": sb(24, F32), "n1": sb(24, F32), "n2": sb(24, F32), "n3": sb(24, F32), "n4": sb(24, F32), "n5": sb(24, F32), "n6": sb(24, F32),
    "e0": sb(24, F32), "e1": sb(24, F32), "e2": sb(24, F32), "e3": sb(24, F32), "e4": sb(24, F32), "e5": sb(24, F32), "e6": sb(24, F32),
    "f0": sb(24, F32), "f1": sb(24, F32), "f2": sb(24, F32),
    "order": sb(24, U16), "ulist": sb(32, U16),
    "wp": sb(24, U16), "wk": sb(24, U16), "wm": sb(24, U16), "wi0": sb(24, U16), "wi1": sb(24, U16), "wf": sb(24, U16), "wp1": sb(24, U16),
    "lkf": sb(3 * C, F32), "yb": sb(C, F32),
    "uq": sb(128, X4), "us": sb(128, U8), "uqd": sb(512, X4), "usd": sb(512, U8), "vq": sb(128, X4), "vs": sb(128, U8),
    "eq": sb(512, X4), "es": sb(512, U8), "wq": sb(512, X4), "wss": sb(512, U8),
    "qx": sb(C, X4), "sx": sb(C, U8), "qz": sb(C, X4), "sz": sb(C, U8),
}
for _t in range(3):
    SCRATCH.update({"qh%d" % _t: sb(F, X4), "sh%d" % _t: sb(F, U8), "lc%d" % _t: sb(F, X4), "ls%d" % _t: sb(F, U8),
                    "pin%d" % _t: sb(24, U16), "mo%d" % _t: sb(12, U16)})
PSUM = ["ps%d" % b for b in range(4)] + ["pw%d" % b for b in range(4)]
SCRATCH.update({n: ("psum", [128, 512], F32) for n in PSUM})

LOADS = ["dx", "du", "dp", "dd", "dk", "dl", "dw", "ds", "dv"]
STORES = ["so1", "so0", "sy1", "sy0", "sl"]
SEMAPHORES = (["qv", "qs", "qt", "qg"] + LOADS + STORES
              + ["%s%d" % (k, t) for t in range(3) for k in ("ap", "am", "ac", "as", "lp", "lm", "lc", "ls")])
COLS = ["qf", "qf2", "q24", "q0", "dec", "thr", "bia", "mark", "lift", "lifs", "quarter"]
COUNTER = {"v": "qv", "s": "qs", "t": "qt", "g": "qg"}


def rank_program(g, core, T, topo):
    rank = T.rank_of(core)
    if rank is None:
        return
    N = len(T.cores)
    OP, AF = AluOpType, ActivationFunctionType
    eng = {"v": g.vector, "s": g.scalar, "t": g.tensor, "g": g, "y": g.sync}

    total, known = {}, {q: {} for q in eng}
    hist, spans = {}, {}

    def cols(r):
        k = (r[1], r[2], r[3])
        if k not in spans:
            spans[k] = sum(1 << i for i in range(r[1], r[2], r[3]))
        return spans[k]

    def V(name, a=0, b=None, st=1):
        return (name, a, SCRATCH[name][1][1] if b is None else b, st)

    def ap(r):
        return T[r[0]][:, r[1]:r[2]] if r[3] == 1 else T[r[0]][:, r[1]:r[2]:r[3]]

    def by(r, off):
        return ap(r).indirect(ap(off))

    def record(rd, wr, op):
        for rs, w in ((rd, 0), (wr, 1)):
            for r in rs:
                hist.setdefault(r[0], []).append((cols(r), w, op))

    def waits(q, rd, wr, sem):
        need = {}
        for rs, w in ((rd, 0), (wr, 1)):
            for r in rs:
                m, bank = cols(r), r[0] in PSUM
                for hm, hw, op in hist.get(r[0], ()):
                    osem, oval, oq, clock = op
                    if not (w or hw or (bank and oq != q)) or not (bank or hm & m):
                        continue
                    if oq == q and osem == COUNTER.get(q) and not hw:
                        continue
                    if osem == sem and sem not in COUNTER.values():
                        continue
                    if known[q].get(osem, 0) < oval and need.get(osem, (0, None))[0] < oval:
                        need[osem] = (oval, clock)
        for osem in sorted(need):
            oval = need[osem][0]
            if any(k != osem and c[1].get(osem, 0) >= oval for k, c in need.items()):
                continue
            eng[q].wait_ge(T.sem[osem], oval if osem in COUNTER.values() else total[osem])
        for osem, (oval, clock) in need.items():
            for k, v in clock.items():
                known[q][k] = max(known[q].get(k, 0), v)
            known[q][osem] = max(known[q].get(osem, 0), oval)

    def do(q, call, rd, wr, sem=None, inc=1):
        sem = sem or COUNTER[q]
        waits(q, rd, wr, sem)
        call(eng[q]).then_inc(T.sem[sem], inc)
        total[sem] = total.get(sem, 0) + inc
        clock = dict(known[q])
        clock[sem] = total[sem]
        record(rd, wr, (sem, total[sem], q, clock))

    def tsc(out, a, s1, op0, s2=None, op1=None, win=None):
        rd = [a] + [s for s in (s1, s2, win) if isinstance(s, tuple)]
        p1 = ap(s1) if isinstance(s1, tuple) else s1
        src = by(win, a) if win else ap(a)
        if op1 is None:
            do("v", lambda e: e.tensor_scalar(ap(out), src, p1, None, op0), rd, [out])
        else:
            do("v", lambda e: e.tensor_scalar(ap(out), src, p1, s2, op0, op1), rd, [out])

    def tt(out, a, b, op, off=None):
        src = by(a, off) if off else ap(a)
        do("v", lambda e: e.tensor_tensor(ap(out), src, ap(b), op), [a, b] + ([off] if off else []), [out])

    def copy(out, a, off=None):
        src = by(a, off) if off else ap(a)
        do("v", lambda e: e.tensor_copy(ap(out), src), [a] + ([off] if off else []), [out])

    def act(out, a, func=AF.Copy, scale=None, off=None, bias=None):
        src = by(a, off) if off else ap(a)
        kw = {} if scale is None else {"scale": scale}
        if bias is not None:
            kw["bias"] = ap(bias) if isinstance(bias, tuple) else bias
        do("s", lambda e: e.activation(ap(out), src, func, **kw), [a] + [r for r in (off, bias) if isinstance(r, tuple)], [out])

    def scan(out, a, b, initial, op0, op1):
        do("v", lambda e: e.tensor_tensor_scan(ap(out), ap(a), ap(b), initial, op0, op1), [a, b], [out])

    def quant(c, s, t):
        do("v", lambda e: e.quantize_mx(ap(c), ap(s), ap(t)), [t], [c, s])

    def mm(out, c, s, c2, s2):
        do("t", lambda e: e.matmul_mx(ap(out), ap(c), ap(s), ap(c2), ap(s2), True, True), [c, s, c2, s2], [out])

    def load(q, sem, out, src, name):
        do(q, lambda e: e.dma_start(out, src), [], [name], sem, 16)

    def store(q, sem, out, src, r):
        do(q, lambda e: e.dma_start(out, src), [r], [], sem, 16)

    def hold(out, row, m, k):
        scan(out, row, V(m, row[1] % C, row[1] % C + row[2] - row[1]), k, OP.min, OP.subtract)

    def last(r):
        return V(r, 15, C, 16)

    def col(name):
        i = COLS.index(name)
        return V("qf", i, i + 1)

    def send(t, kind, dst, out, src, codes=False):
        rid, pid, _ = topo.addr(dst)
        o, i = (ap(out).bitcast(dt.uint8), ap(src).bitcast(dt.uint8)) if codes else (ap(out), ap(src))
        lsem = "l%s%d" % (kind, t)
        waits("g", [src], [], lsem)
        g.remote_dma(o, i, T.sem["a%s%d" % (kind, t)], T.sem[lsem], pid, rid, topo.mask(core, dst))
        total[lsem] = len(topo.engines(core, dst))
        clock = dict(known["g"])
        clock[lsem] = total[lsem]
        record([src], [], (lsem, total[lsem], "r", clock))

    for t in range(3):
        srank, drank = T.cores[(rank - STEP[t]) % N], T.cores[(rank + STEP[t]) % N]
        for kind, frm, b in (("p", drank, "pin"), ("m", srank, "mo"), ("c", srank, "lc"), ("s", srank, "ls")):
            s, n = "a%s%d" % (kind, t), len(topo.engines(frm, core))
            total[s] = n
            record([], [V("%s%d" % (b, t))], (s, n, "r", {s: n}))

    load("y", "dl", ap(V("lw")), T.pl[:, :], V("lw"))
    load("s", "du", ap(V("ut")), T.u[:, :], V("ut"))
    load("y", "dx", ap(V("xt")), T.x[:, :], V("xt"))
    for k, (q, sem, inp) in enumerate((("y", "dp", T.pl), ("s", "dd", T.dl), ("y", "dk", T.kl))):
        r = V("li", k * C, k * C + C)
        for i in range(16):
            load(q, sem, T.li[i:128:16, k * C:k * C + C], inp[:, :], r)
    load("y", "dw", T.wq[:, :].bitcast(dt.uint8), T.wc[:, :], V("wq"))
    load("y", "ds", ap(V("wss")), T.ws[:, :], V("wss"))
    load("y", "dv", ap(V("vt")), T.v[:, :], V("vt"))

    def iota(out, pattern, cm, flag=True):
        kw = {"allow_small_or_imprecise_dtypes": True} if flag else {}
        do("g", lambda e: e.iota(ap(out), pattern, 0, cm, **kw), [], [out])

    iota(V("itp"), [[0, 2]], 1, False)
    iota(V("itu"), [[1, 4], [16, 8]], 0)
    iota(V("itk"), [[1, 24]], 0)
    iota(V("itt"), [[0, 24], [1, 16]], 0)
    iota(V("itc"), [[16, 24]], 0)
    do("v", lambda e: e.memset(ap(V("ones")), 1.0), [], [V("ones")])
    do("v", lambda e: e.memset(T.ta[:, NB:NB + 1], 192.0), [], [V("ta", NB, NB + 1)])
    do("v", lambda e: e.memset(T.ta[:, NN:2704], 576.0), [], [V("ta", NN, 2704)])
    tsc(V("itq"), V("itp"), 15, OP.bitwise_and)
    copy(V("qf", 0, 2), V("itq"))
    tsc(col("quarter"), col("qf"), 0.0, OP.mult, 0.25, OP.add)
    tsc(col("q0"), col("qf"), 0.0, OP.is_equal)
    copy(V("ulist"), V("itu"))
    tsc(col("q24"), col("qf"), 24.0, OP.mult)
    tsc(V("order"), V("itk"), col("q24"), OP.add)
    tsc(col("lifs"), col("q0"), 8.0, OP.mult)
    tsc(col("dec"), col("q0"), -2.0 * OFF, OP.mult, 192.0 + OFF, OP.add)
    tsc(col("thr"), col("q0"), 8.0, OP.mult, -3.5, OP.add)
    tsc(col("bia"), col("q0"), -8.0, OP.mult, 4.0, OP.add)
    tsc(col("mark"), col("q0"), 2.0 * OFF, OP.mult, 191.5 - OFF, OP.add)
    tsc(col("lift"), col("q0"), 2.0 * OFF, OP.mult)
    for b in range(4):
        o = V("et", 512 * b, 512 * b + 512)
        do("g", lambda e: e.affine_select(ap(o), ap(V("ones")), [[-1, 512]], OP.is_equal, 0.0, b, 4), [V("ones")], [o])
    act(V("m1"), V("itt"), AF.Sign, scale=-1.0, bias=col("qf"))
    act(V("m2"), V("m1"), AF.Square, bias=col("quarter"))
    act(V("mb"), V("m2"), scale=-2.0 * OFF, bias=1.125 * OFF)
    act(V("ms"), V("m2"), scale=-8.0, bias=4.5)
    copy(V("wp"), V("lw"))
    quant(V("uq"), V("us"), V("ut"))
    do("v", lambda e: e.tensor_copy(T.uqd[:, 0:512].bitcast(dt.uint32), T.uq[:, 0:128].bitcast(dt.uint32).indirect(T.ulist[:, 0:32])),
       [V("uq"), V("ulist")], [V("uqd")])
    act(V("usd"), V("us"), off=V("ulist"))
    def constants():
        tsc(V("c24"), V("itc"), col("qf"), OP.add)
        tsc(last("ms"), last("ms"), col("lifs"), OP.subtract)
        tsc(V("l0"), V("c24"), 2.0 * C, OP.add)
        tsc(last("mb"), last("mb"), col("lift"), OP.subtract)

    def prep(a, e, onv, rest=None):
        x, sx = V("qx", a, e), V("sx", a, e)
        quant(x, sx, V("xt", 4 * a, 4 * e))
        for i in range(4):
            mm(V("ps%d" % i, 0, e - a), V("uqd", 128 * i, 128 * i + 128), V("usd", 128 * i, 128 * i + 128), x, sx)
        for b in range(4):
            o, i = V("xh", C * b + a, C * b + e), V("xt", 4 * a + b, 4 * e, 4)
            if b in onv:
                tsc(o, i, 0.5, OP.mult)
            else:
                act(o, i, scale=0.5)
        if rest:
            rest()
        tsc(V("a0", a, e), V("ps0", 0, e - a), 0.0, OP.is_gt)
        for i in range(1, 4):
            if a or i != 2:
                act(V("sg%d" % i, a, e), V("ps%d" % i, 0, e - a), AF.Sign)

    def early():
        for i in (2, 3):
            hold(V("sc%d" % i, F, C), V("sg%d" % i, F, C), "ms", 8.0)

    def ahead_rows(both=False):
        (copy if both else act)(V("ppr"), V("ta", 0, C), off=V("wp"))
        act(V("dpr"), V("ta", 2 * C, 3 * C), off=V("wp"))

    def ahead():
        hold(V("scx"), V("ppr"), "mb", 2.0 * OFF)
        hold(V("scy"), V("dpr"), "mb", 2.0 * OFF)
        tsc(V("pf"), last("scx"), col("dec"), OP.add)
        tsc(V("df"), last("scy"), col("dec"), OP.add)
        tt(V("zd"), V("pf"), V("df"), OP.subtract)
        tt(V("yc"), V("df"), V("l0"), OP.subtract)
        tsc(V("zc"), V("zd"), float(C), OP.add)

    def aside(out, a):
        do("g", lambda e: e.affine_select(ap(out), ap(a), [[1, C]], OP.is_ge, 0.0, 0, 0), [a], [out])

    def rows(k):
        tsc(V("ta", 2 * C * k, 2 * C * k + C), V("order"), -192.0, OP.add, win=V("li", C * k, C * k + C))

    def turn(t):
        copy(V("ga"), V("a0"), off=V("wp"))
        act(V("gb"), V("sg1"), off=V("wp"))
        n = F if t else C
        if t:
            tsc(V("sg2", 0, n), V("ps2", 0, n), 0.0, OP.is_gt)
        else:
            act(V("sg2"), V("ps2", 0, n), AF.Sign)
            rows(0)
            rows(1)
            ahead_rows()
            rows(2)
        hold(V("sca"), V("ga"), "ms", 8.0)
        hold(V("sc2", 0, n), V("sg2", 0, n), "ms", 8.0)
        tsc(V("n0"), last("sca"), col("thr"), OP.is_ge)
        hold(V("sc3", 0, n), V("sg3", 0, n), "ms", 8.0)
        for i in (0, 1):
            act(V("e%d" % i), last("sc%d" % (i + 2)), AF.Relu, bias=col("bia"))
        act(V("e2"), V("e1"), AF.Copy, scale=-767.0, bias=2.0 * C - NN)
        act(V("e3"), V("e1"), AF.Copy, scale=-1.0, bias=1.0 * NN)
        if t == 0:
            for a, b in ((1, 0), (3, 2), (5, 4)):
                act(V("ta", C * a, C * a + C), V("ta", C * b, C * b + C))
            for n, a, b in (("ta", 6, 0), ("tb", 1, 0), ("tb", 3, 2), ("tb", 5, 4)):
                aside(V(n, C * a, C * a + C), V("ta", C * b, C * b + C))
            ahead()
        tt(V("n1"), V("n0"), V("yc"), OP.mult)
        tt(V("n2"), V("n0"), V("zc"), OP.mult)
        tt(V("n3"), V("n1"), V("l0"), OP.add)
        tsc(V("n4"), V("n2"), -1.0 * C, OP.add)
        hold(V("scb"), V("gb"), "ms", 8.0)
        tt(V("e4"), V("e0"), V("e2"), OP.mult)
        tsc(V("n5"), last("scb"), col("thr"), OP.is_ge)
        tt(V("e5"), V("e4"), V("e3"), OP.add)
        tt(V("n1"), V("n5"), V("n4"), OP.mult)
        tt(V("n6"), V("n1"), V("n3"), OP.add)
        tt(V("e6"), V("e0"), V("n6"), OP.mult)
        copy(V("wi0"), V("n6"))
        tt(V("e4"), V("e6"), V("e5"), OP.add)
        copy(V("wf"), V("e4"))
        copy(V("tb", 0, C), V("ta", 0, 3 * C), off=V("wi0"))
        act(V("fr"), V("ta", 0, 2704), off=V("wf"))
        act(V("tb", 2 * C, 3 * C), V("ta", 2 * C, 5 * C), off=V("wi0"))
        hold(V("scp"), V("tb", 0, C), "mb", 2.0 * OFF)
        tsc(V("wp1"), last("scp"), col("dec"), OP.add)
        aside(V("tb", 6 * C, 7 * C), V("tb", 0, C))
        act(V("tb", 4 * C, 5 * C), V("ta", 4 * C, 7 * C), off=V("wi0"))
        copy(V("gf"), V("fr"), off=V("wp1"))
        hold(V("scf"), V("gf"), "mb", 2.0 * OFF)
        tsc(V("f0"), last("scf"), col("mark"), OP.is_ge)
        tt(V("f1"), V("f0"), V("c24"), OP.mult)
        tt(V("f2"), last("scf"), V("f1"), OP.add)
        tsc(V("wi1"), V("f2"), col("dec"), OP.add)
        copy(V("ta", 0, C), V("tb", 0, 3 * C), off=V("wi1"))
        act(V("ta", 4 * C, 5 * C), V("tb", 4 * C, 7 * C), off=V("wi1"))
        hold(V("scp"), V("ta", 0, C), "mb", 2.0 * OFF)
        tsc(V("wp"), last("scp"), col("dec"), OP.add)

    constants()
    prep(0, C, (0, 1))

    for t in range(3):
        src, dst = T.cores[(rank - STEP[t]) % N], T.cores[(rank + STEP[t]) % N]
        turn(t)
        send(t, "p", src, V("pin%d" % t), V("wp"))
        hold(V("scx"), V("ta", 4 * C, 5 * C), "mb", 2.0 * OFF)
        tsc(V("wk"), last("scx"), col("dec"), OP.add)

        def zpart(lo, hi):
            for b in range(4):
                z, x = V("zp", 4 * lo + (hi - lo) * b, 4 * lo + (hi - lo) * (b + 1)), V("xh", C * b, C * b + C)
                act(z, x, off=V("wp", lo // 16, hi // 16))
                tt(V("zt", 4 * lo + b, 4 * hi, 4), x, z, OP.add, off=V("wk", lo // 16, hi // 16))
            quant(V("qz", lo, hi), V("sz", lo, hi), V("zt", 4 * lo, 4 * hi))

        def wpart(lo, hi):
            for b in range(4):
                mm(V("pw%d" % b, 0, hi - lo), V("wq", 128 * b, 128 * b + 128), V("wss", 128 * b, 128 * b + 128), V("qz", lo, hi), V("sz", lo, hi))

        def hpart(lo, hi, b, on):
            o, i = V("hh", C * b + lo, C * b + hi), V("pw%d" % b, 0, hi - lo)
            if on == "v":
                tsc(o, i, 0.03125, OP.mult)
            else:
                act(o, i, scale=0.03125)

        zpart(*BLOCKS[0])
        wpart(*BLOCKS[0])
        zpart(*BLOCKS[1])
        for b in range(4):
            hpart(*BLOCKS[0], b, "v" if b == 3 else "s")
        for lo, hi in ((F, C), (0, F)):
            act(V("mr", lo, hi), V("ta", 4 * C, 5 * C), off=V("pin%d" % t, lo // 16, hi // 16))
        wpart(*BLOCKS[1])
        hpart(*BLOCKS[1], 0, "v")
        hold(V("scy", F, C), V("mr", F, C), "mb", 2.0 * OFF)
        hpart(*BLOCKS[1], 1, "v")
        tsc(V("wm", 12, 24), V("scy", F + 15, C, 16), col("dec"), OP.add)
        send(t, "m", dst, V("mo%d" % t), V("wm", 12, 24))
        hpart(*BLOCKS[1], 2, "v")
        hold(V("scy", 0, F), V("mr", 0, F), "mb", 2.0 * OFF)
        tsc(V("wm", 0, 12), V("scy", 15, F, 16), col("dec"), OP.add)
        hpart(*BLOCKS[1], 3, "s")
        for b in range(4):
            o, x, off = V("ft", b, 4 * F, 4), V("hh", C * b, C * b + C), V("wm", 0, 12)
            if b >= 2:
                copy(o, x, off)
            else:
                act(o, x, off=off)
        quant(V("qh%d" % t), V("sh%d" % t), V("ft"))
        send(t, "c", dst, V("lc%d" % t), V("qh%d" % t), True)
        send(t, "s", dst, V("ls%d" % t), V("sh%d" % t))
        act(V("ta", 2 * C, 3 * C), V("tb", 2 * C, 5 * C), off=V("wi1"))
        if t == 0:
            quant(V("eq"), V("es"), V("et"))
        if t < 2:
            ahead_rows(True)
        else:
            quant(V("vq"), V("vs"), V("vt"))
            for k in (0, 2, 1):
                tsc(V("lkf", C * k, C * k + C), V("ta", 2 * C * k, 2 * C * k + C), 192.0, OP.add)
            store("y", "sl", T.lk[:, :], T.lkf[0:128:16, 0:3 * C], V("lkf"))
        for b in range(4):
            x = V("xt", 4 * F + b, 4 * C, 4)
            tt(x, V("hh", C * b, C * b + C), x, OP.add, off=V("mo%d" % t))
        if t < 2:
            prep(F, C, (), ahead)
            early()
            act(V("ta", 6 * C, 7 * C), V("ta", 0, C))
        else:
            quant(V("qx", F, C), V("sx", F, C), V("xt", 4 * F, 4 * C))
            mm(V("ps1", 0, F), V("vq"), V("vs"), V("qx", F, C), V("sx", F, C))
            act(V("yb", F, C), V("ps1", 0, F))
            store("y", "so1", T.oc[:, 4 * F:4 * C], T.qx[:, F:C].bitcast(dt.uint8), V("qx", F, C))
            for k in range(4):
                store("y", "so1", T.osc[4 * k:4 * k + 4, F:C], T.sx[32 * k:32 * k + 4, F:C], V("sx", F, C))
            store("y", "sy1", T.y[:, F:C], ap(V("yb", F, C)), V("yb", F, C))
        for b in range(4):
            mm(V("pw%d" % b, 0, F), V("eq", 128 * b, 128 * b + 128), V("es", 128 * b, 128 * b + 128), V("lc%d" % t), V("ls%d" % t))
        for b in range(4):
            x = V("xt", b, 4 * F, 4)
            tt(x, V("pw%d" % b, 0, F), x, OP.add)
        if t < 2:
            prep(0, F, (0, 1))
    quant(V("qx", 0, F), V("sx", 0, F), V("xt", 0, 4 * F))
    mm(V("ps0", 0, F), V("vq"), V("vs"), V("qx", 0, F), V("sx", 0, F))
    act(V("yb", 0, F), V("ps0", 0, F))
    store("y", "so0", T.oc[:, 0:4 * F], T.qx[:, 0:F].bitcast(dt.uint8), V("qx", 0, F))
    for k in range(4):
        store("s" if k % 2 else "y", "so0", T.osc[4 * k:4 * k + 4, 0:F], T.sx[32 * k:32 * k + 4, 0:F], V("sx", 0, F))
    store("y", "sy0", T.y[:, 0:F], ap(V("yb", 0, F)), V("yb", 0, F))
    for s in sorted(total):
        g.wait_ge(T.sem[s], total[s])
